import numpy as np
import ml_dtypes


def mxq(x, axis, fmt="e4m3"):
    dtype, down = {"e4m3": (ml_dtypes.float8_e4m3fn, 7), "e5m2": (ml_dtypes.float8_e5m2, 14)}[fmt]
    v = np.moveaxis(np.asarray(x, np.float32).astype(ml_dtypes.bfloat16).astype(np.float64), axis, -1)
    blocks = v.reshape(v.shape[:-1] + (-1, 32))
    amax = np.abs(blocks).max(-1, keepdims=True)
    byte = np.maximum(np.where(amax > 0, np.frexp(amax)[1] - 1 + 127, 0) - down, 1)
    scale = np.exp2(byte - 127.0)
    codes = (blocks / scale).astype(np.float32).astype(dtype).astype(np.float64)
    return np.moveaxis((codes * scale).reshape(v.shape), -1, axis)


WIDE = False


def mx_kscale(k):
    if not WIDE:
        return np.ones(k)
    levels = np.array([10, -10, 5, -5, 0])
    if k % 512:
        return np.exp2(np.random.permutation(np.resize(levels, k // 32))).repeat(32)
    a = np.empty((k // 512, 16))
    for p in range(k // 512):
        a[p, :8] = np.random.permutation(np.resize(levels, 8))
        for g in range(8):
            far = levels[np.abs(levels - a[p, g]) >= 10]
            a[p, g + 8] = far[np.random.randint(len(far))]
    return np.exp2(a.ravel()).repeat(32)


BF16 = ml_dtypes.bfloat16


def bf(x):
    return np.asarray(x, np.float32).astype(BF16)


def f64(x):
    return np.asarray(x).astype(np.float64)


E2M1 = np.array([0.0, 0.5, 1.0, 1.5, 2.0, 3.0, 4.0, 6.0, -0.0, -0.5, -1.0, -1.5, -2.0, -3.0, -4.0, -6.0])


def pack_weight(w, fmt):
    k, n = w.shape
    w = f64(bf(w)).reshape(k // 32, 32, n)
    amax = np.abs(w).max(1)
    if fmt == "e4m3":
        byte = np.frexp(amax)[1] - 1 + 127 - 7
    else:
        mant, ex = np.frexp(amax / 6.0)
        byte = np.where(mant > 0.5, ex, ex - 1) + 127
    byte = np.clip(np.where(amax > 0, byte, 1), 1, 254)
    scaled = (w * np.exp2(127.0 - byte)[:, None, :]).reshape(k, n).astype(np.float32)
    by_word = np.ascontiguousarray(scaled.reshape(k // 512, 128, 4, n).transpose(0, 1, 3, 2))
    if fmt == "e4m3":
        words = by_word.astype(ml_dtypes.float8_e4m3fn).view(np.uint8)
    else:
        c = by_word.astype(ml_dtypes.float4_e2m1fn).view(np.uint8) & 0xF
        words = c[..., 0::2] | (c[..., 1::2] << 4)
    return np.ascontiguousarray(words), np.ascontiguousarray(byte.astype(np.uint8).reshape(k // 512, 16, n))


def unpack_weight(words, scales, fmt):
    g, p, n, _ = words.shape
    if fmt == "e4m3":
        vals = np.ascontiguousarray(words).view(ml_dtypes.float8_e4m3fn).astype(np.float64)
    else:
        nib = np.empty((g, p, n, 4), np.uint8)
        nib[..., 0::2] = words & 0xF
        nib[..., 1::2] = words >> 4
        vals = E2M1[nib]
    vals = vals * np.repeat(np.exp2(scales.astype(np.float64) - 127.0), 8, axis=1)[..., None]
    return vals.transpose(0, 1, 3, 2).reshape(g * 512, n)
def pack4(w):
    words, scales = pack_weight(w, "e2m1")
    return words.reshape(words.shape[0], 128, -1), scales


def unpack4(words, scales):
    return unpack_weight(words.reshape(words.shape[0], 128, -1, 2), scales, "e2m1")


K, T, F, C = 1024, 2048, 1024, 512


def setup_inputs():
    s = mx_kscale(K)
    t = mx_kscale(F)
    x_words, x_scales = pack4(np.random.standard_normal((K, T)) * s[:, None])
    bank_words, bank_scales = pack4(np.random.standard_normal((K, F)) / np.sqrt(K) / s[:, None])
    mix_words, mix_scales = pack_weight(np.random.standard_normal((F, C)) / np.sqrt(F) / t[:, None], "e4m3")
    return {"x_words": x_words, "x_scales": x_scales,
            "bank_words": bank_words, "bank_scales": bank_scales,
            "gain": bf((1 + 0.1 * np.random.standard_normal(F)) * t),
            "mix_words": mix_words, "mix_scales": mix_scales,
            "bias": bf(0.3 * np.random.standard_normal(C))}


def reference(x_words, x_scales, bank_words, bank_scales, gain, mix_words, mix_scales, bias):
    x = unpack4(x_words, x_scales)
    bank = unpack4(bank_words, bank_scales)
    mix = unpack_weight(mix_words, mix_scales, "e4m3")
    y = bank.T @ x
    h = np.abs(y) * f64(gain)[:, None]
    z = mix.T @ mxq(h, 0, "e4m3")
    return z + f64(bias)[:, None]

@@ -1,0 +1,342 @@
+from contextlib import ExitStack
+
+import concourse.mybir as mybir
+
+SAMPLES, FRAMES, FILTERS, CHANNELS = 1024, 2048, 1024, 512
+FLOPS = 2 * SAMPLES * FRAMES * FILTERS + 2 * FILTERS * FRAMES * CHANNELS
+
+F32 = mybir.dt.float32
+BF16 = mybir.dt.bfloat16
+I32 = mybir.dt.int32
+U32 = mybir.dt.uint32
+U8 = mybir.dt.uint8
+FP8X4 = mybir.dt.float8_e4m3fn_x4
+FP4X4 = mybir.dt.float4_e2m1fn_x4
+ALU = mybir.AluOpType
+ACT = mybir.ActivationFunctionType
+
+P = 128
+PACK = 4
+K_PASS = P * PACK
+PASSES = 2
+X_TILE = 512
+CHUNKS = [(0, 512), (512, 512), (1024, 512), (1536, 512)]
+F_TILES = FILTERS // P
+C_TILES = CHANNELS // P
+WARM = 36
+K0, RN, RD = 14, 1, 2
+VECTOR_UNITS = ((3,), 4)
+X_HEAD = 1024
+W_COLS = 128
+
+
+def tile_filter_bank_channel_mixer_s4_kernel(
+    tc, x_words, x_scales, bank_words, bank_scales, gain, mix_words, mix_scales, bias, out
+):
+    nc = tc.nc
+    with ExitStack() as ctx:
+        keep = ctx.enter_context(tc.tile_pool(name="keep", bufs=1))
+        work = ctx.enter_context(tc.tile_pool(name="work", bufs=3))
+        psum = ctx.enter_context(tc.psum_pool(name="psum", bufs=4))
+        ctx.enter_context(nc.allow_non_contiguous_dma(reason="small gain and bias columns"))
+        ctx.enter_context(tc.manual_schedule())
+
+        x_sb = []
+        for j in range(FRAMES // X_TILE):
+            xt = keep.tile([P, PASSES, 2 * X_TILE], U8, name="x%d" % j, align_bytes=64)
+            x_sb.append(xt)
+        b_raw = []
+        for h in range(2):
+            bt = keep.tile([P, PASSES, 2 * K_PASS], U8, name="braw%d" % h, align_bytes=64)
+            b_raw.append(bt)
+        b_sb, bs_sb = [], []
+        for f in range(F_TILES):
+            bt = keep.tile([P, PASSES, 2 * P], U8, name="b%d" % f, align_bytes=64)
+            b_sb.append(bt)
+            st = keep.tile([P, PASSES, P], U8, name="bs%d" % f, align_bytes=64)
+            bs_sb.append(st)
+        m_sb = keep.tile([P, PASSES, 4 * CHANNELS], U8, name="mixw", align_bytes=64)
+        bs_raw = keep.tile([P, PASSES * FILTERS], U8, name="bsraw", align_bytes=64)
+        xs_head = keep.tile([P, PASSES * X_HEAD], U8, name="xshead", align_bytes=64)
+        xs_rest = keep.tile([P, PASSES * (FRAMES - X_HEAD)], U8, name="xsrest", align_bytes=64)
+        ms = keep.tile([P, PASSES * CHANNELS], U8, name="ms", align_bytes=64)
+        gain_bf = keep.tile([P, F_TILES], BF16, name="gainbf")
+        gain_f = keep.tile([P, F_TILES], F32, name="gainf")
+        sgn = keep.tile([P, F_TILES], F32, name="sgn")
+        bias_bf = keep.tile([P, C_TILES, 2], BF16, name="biasbf")
+        warm = keep.tile([P, 4 * W_COLS], BF16, name="warm", align_bytes=64)
+        warm_c = keep.tile([P, W_COLS], U32, name="warmc", align_bytes=64)
+        warm_s = keep.tile([P, W_COLS], U8, name="warms", align_bytes=64)
+        dummy = keep.tile([P, 1], F32, name="dummy")
+
+        def load_bank(eng, h):
+            eng.dma_start(
+                out=b_raw[h][:].bitcast(I32),
+                in_=bank_words[:, :, 2 * K_PASS * h : 2 * K_PASS * (h + 1)].rearrange("g p b -> p g b").bitcast(I32),
+            )
+
+        def load_x(eng, j):
+            eng.dma_start(
+                out=x_sb[j][:].bitcast(I32),
+                in_=x_words[:, :, 2 * X_TILE * j : 2 * X_TILE * (j + 1)].rearrange("g p b -> p g b").bitcast(I32),
+            )
+
+        def load_scales(eng, tile, src, r):
+            eng.dma_start(
+                out=tile[r:P:32, :].rearrange("p (g n) -> p g n", g=PASSES).bitcast(I32),
+                in_=src.rearrange("g (q r) n -> r q g n", r=4)[r].bitcast(I32),
+            )
+
+        nc.gpsimd.memset(bs_raw[:].bitcast(I32), 0)
+        nc.vector.memset(xs_head[:].bitcast(I32), 0)
+        nc.gpsimd.memset(warm[:].bitcast(U32), 0x3F803F80)
+        nc.vector.quantize_mx(out=warm_c[:].bitcast(FP8X4), scales=warm_s[:], in_=warm[:])
+        for u in range(WARM):
+            wz = psum.tile([P, W_COLS], F32, name="z", tag="z", bufs=4)
+            nc.tensor.matmul_mx(
+                out=wz[:],
+                lhsT=warm_c[:, 0:P].bitcast(FP8X4),
+                lhsT_scale=warm_s[:, 0:P],
+                rhs=warm_c[:].bitcast(FP8X4),
+                rhs_scale=warm_s[:],
+                start=True,
+                stop=True,
+            )
+        nc.vector.memset(xs_rest[:].bitcast(I32), 0)
+        nc.vector.memset(ms[:].bitcast(I32), 0)
+        nc.vector.memset(dummy[:], 0.0)
+        nc.scalar.activation(out=dummy[:], in_=dummy[:], func=ACT.Abs)
+
+        nc.sync.dma_start(
+            out=gain_bf[:].rearrange("p (h t) -> p h t", t=PACK), in_=gain.rearrange("(h p t) -> p h t", p=P, t=PACK)
+        )
+        for r in range(4):
+            load_scales(nc.sync, bs_raw, bank_scales, r)
+        load_bank(nc.sync, 0)
+        for r in range(1):
+            load_scales(nc.sync, xs_head, x_scales[:, :, 0:X_HEAD], r)
+        load_x(nc.sync, 0)
+        for r in range(1, 4):
+            load_scales(nc.sync, xs_head, x_scales[:, :, 0:X_HEAD], r)
+        load_bank(nc.sync, 1)
+        load_x(nc.sync, 1)
+        for r in range(4):
+            load_scales(nc.sync, ms, mix_scales, r)
+        for r in range(4):
+            load_scales(nc.sync, xs_rest, x_scales[:, :, X_HEAD:FRAMES], r)
+        nc.sync.dma_start(out=m_sb[:], in_=mix_words.rearrange("g p n t -> p g (n t)"))
+        nc.sync.dma_start(
+            out=bias_bf[:, :, 0:1], in_=bias.rearrange("(c p o) -> p c o", p=P, o=1)
+        )
+        load_x(nc.sync, 2)
+        load_x(nc.sync, 3)
+
+        def permute_codes(f):
+            h, t = divmod(f, PACK)
+            nc.vector.tensor_copy(
+                out=b_sb[f][:].rearrange("p g (m b) -> p g m b", b=2),
+                in_=b_raw[h][:].rearrange("p g (m t b) -> p t g m b", t=PACK, b=2)[:, t],
+            )
+
+        def permute_scales(f):
+            h, t = divmod(f, PACK)
+            nc.vector.tensor_copy(
+                out=bs_sb[f][:],
+                in_=bs_raw[:].rearrange("p (g h m t) -> p h t g m", g=PASSES, h=2, t=PACK)[:, h, t],
+            )
+
+        sub = {}
+        ymap = {}
+        grouped = {}
+        codes = {}
+        zmap = {}
+
+        def x_scale_columns(g, n0, w):
+            if n0 < X_HEAD:
+                return xs_head[:, g * X_HEAD + n0 : g * X_HEAD + n0 + w]
+            start = g * (FRAMES - X_HEAD) + n0 - X_HEAD
+            return xs_rest[:, start : start + w]
+
+        def bank_pass(i, f):
+            n0, w = CHUNKS[i]
+            j, o = divmod(n0, X_TILE)
+            y = psum.tile([P, w], F32, name="y", tag="y", bufs=4)
+            for g in range(PASSES):
+                nc.tensor.matmul_mx(
+                    out=y[:],
+                    lhsT=b_sb[f][:, g, :].bitcast(FP4X4),
+                    lhsT_scale=bs_sb[f][:, g, :],
+                    rhs=x_sb[j][:, g, 2 * o : 2 * (o + w)].bitcast(FP4X4),
+                    rhs_scale=x_scale_columns(g, n0, w),
+                    start=(g == 0),
+                    stop=(g == PASSES - 1),
+                )
+            ymap[(i, f)] = y
+
+        def rectify(i, f):
+            h, t = divmod(f, PACK)
+            w = CHUNKS[i][1]
+            if t == 0:
+                s = work.tile([P, PACK, w], BF16, name="s", tag="s", bufs=4, align_bytes=64)
+                sub[(i, h)] = s
+            nc.scalar.activation(
+                out=sub[(i, h)][:, t, :], in_=ymap[(i, f)][:], func=ACT.Abs, scale=gain_f[:, f : f + 1]
+            )
+
+        def sign(i, f):
+            h, t = divmod(f, PACK)
+            nc.vector.tensor_scalar(
+                out=sub[(i, h)][:, t, :], in0=sub[(i, h)][:, t, :], scalar1=sgn[:, f : f + 1], scalar2=None, op0=ALU.mult
+            )
+
+        def interleave(i, h):
+            w = CHUNKS[i][1]
+            gr = work.tile([P, w, PACK], BF16, name="gr", tag="gr", bufs=3, align_bytes=64)
+            nc.vector.tensor_copy(
+                out=gr[:].rearrange("p (c i) t -> p c t i", i=4), in_=sub[(i, h)][:].rearrange("p t (c i) -> p c t i", i=4)
+            )
+            grouped[(i, h)] = gr
+
+        def quantize(i, h):
+            w = CHUNKS[i][1]
+            c = work.tile([P, w], U32, name="hc", tag="hc", bufs=6, align_bytes=64)
+            sc = work.tile([P, w], U8, name="hs", tag="hs", bufs=6, align_bytes=64)
+            nc.vector.quantize_mx(
+                out=c[:].bitcast(FP8X4), scales=sc[:], in_=grouped[(i, h)][:].rearrange("p n t -> p (n t)")
+            )
+            codes[(i, h)] = (c, sc)
+
+        def mix_pass(i, c, g):
+            w = CHUNKS[i][1]
+            if g == 0:
+                z = psum.tile([P, w], F32, name="z", tag="z", bufs=4)
+                zmap[(i, c)] = z
+            hc, hs = codes[(i, g)]
+            nc.tensor.matmul_mx(
+                out=zmap[(i, c)][:],
+                lhsT=m_sb[:, g, 4 * P * c : 4 * P * (c + 1)].bitcast(FP8X4),
+                lhsT_scale=ms[:, g * CHANNELS + P * c : g * CHANNELS + P * (c + 1)],
+                rhs=hc[:].bitcast(FP8X4),
+                rhs_scale=hs[:],
+                start=(g == 0),
+                stop=(g == PASSES - 1),
+            )
+
+        def finish(i, c, on_vector):
+            n0, w = CHUNKS[i]
+            o = work.tile([P, w], F32, name="o", tag="o", bufs=6, align_bytes=64)
+            z = zmap[(i, c)]
+            if on_vector:
+                nc.vector.tensor_scalar(
+                    out=o[:], in0=z[:], scalar1=bias_bf[:, c, 0:1], scalar2=None, op0=ALU.add
+                )
+            else:
+                nc.scalar.activation(out=o[:], in_=z[:], func=ACT.Identity, bias=bias_bf[:, c, 0:1])
+            nc.sync.dma_start(out=out[P * c : P * (c + 1), n0 : n0 + w], in_=o[:])
+
+        for f in range(PACK):
+            permute_codes(f)
+            permute_scales(f)
+        nc.vector.tensor_copy(out=gain_f[:], in_=gain_bf[:])
+        nc.vector.tensor_scalar(out=sgn[:], in0=gain_f[:], scalar1=0.0, scalar2=2.0, op0=ALU.is_ge, op1=ALU.mult)
+        nc.vector.tensor_scalar(out=sgn[:], in0=sgn[:], scalar1=-1.0, scalar2=None, op0=ALU.add)
+
+        order = [(i, f) for i in range(len(CHUNKS)) for f in range(F_TILES)]
+        last = len(CHUNKS) - 1
+        tasks = []
+        fresh = []
+        emitted = 0
+        for k, (i, f) in enumerate(order):
+            bank_pass(i, f)
+            rectify(i, f)
+            tasks += fresh
+            fresh = []
+            if k >= 1:
+                pi, pf = order[k - 1]
+                sign(pi, pf)
+                if pf % PACK == PACK - 1:
+                    fresh = [(interleave, (pi, pf // PACK)), (quantize, (pi, pf // PACK))]
+            if PACK + k < F_TILES:
+                permute_codes(PACK + k)
+                permute_scales(PACK + k)
+            for u in range(2 if len(tasks) > 2 else 1):
+                if tasks:
+                    what, args = tasks.pop(0)
+                    what(*args)
+            mi, c = divmod(emitted, C_TILES)
+            if (k - K0) * RN >= (emitted + 1) * RD and (mi, 1) in codes:
+                emitted += 1
+                for g in range(PASSES):
+                    mix_pass(mi, c, g)
+                if emitted % VECTOR_UNITS[1] in VECTOR_UNITS[0]:
+                    tasks.append((finish, (mi, c, True)))
+                else:
+                    finish(mi, c, False)
+        sign(last, F_TILES - 1)
+        for what, args in tasks:
+            what(*args)
+        half = CHUNKS[last][1] // 2
+        parts = []
+        for e in range(2):
+            gr = work.tile([P, half, PACK], BF16, name="gr", tag="gr", bufs=3, align_bytes=64)
+            nc.vector.tensor_copy(
+                out=gr[:].rearrange("p (c i) t -> p c t i", i=4),
+                in_=sub[(last, 1)][:, :, half * e : half * (e + 1)].rearrange("p t (c i) -> p c t i", i=4),
+            )
+            parts.append(gr)
+        tails = []
+        for e in range(2):
+            hc = work.tile([P, half], U32, name="hc", tag="hc", bufs=6, align_bytes=64)
+            hs = work.tile([P, half], U8, name="hs", tag="hs", bufs=6, align_bytes=64)
+            nc.vector.quantize_mx(
+                out=hc[:].bitcast(FP8X4), scales=hs[:], in_=parts[e][:].rearrange("p n t -> p (n t)")
+            )
+            tails.append((hc[:], hs[:]))
+        for u in range(emitted, last * C_TILES):
+            mi, c = divmod(u, C_TILES)
+            for g in range(PASSES):
+                mix_pass(mi, c, g)
+            finish(mi, c, False)
+        c0, s0 = codes[(last, 0)]
+        ends = {}
+        for g in range(PASSES):
+            for e in range(2):
+                if g == 0:
+                    hc, hs = c0[:, half * e : half * (e + 1)], s0[:, half * e : half * (e + 1)]
+                else:
+                    hc, hs = tails[e]
+                for c in range(C_TILES):
+                    if g == 0:
+                        if e == 0:
+                            z = psum.tile([P, half], F32, name="z", tag="z", bufs=4)
+                        else:
+                            z = psum.tile([P, half], F32, name="y", tag="y", bufs=4)
+                        ends[(e, c)] = z
+                    nc.tensor.matmul_mx(
+                        out=ends[(e, c)][:],
+                        lhsT=m_sb[:, g, 4 * P * c : 4 * P * (c + 1)].bitcast(FP8X4),
+                        lhsT_scale=ms[:, g * CHANNELS + P * c : g * CHANNELS + P * (c + 1)],
+                        rhs=hc.bitcast(FP8X4),
+                        rhs_scale=hs,
+                        start=(g == 0),
+                        stop=(g == PASSES - 1),
+                    )
+        n0 = CHUNKS[last][0]
+        outs = []
+        for c in range(C_TILES):
+            o = work.tile([P, 2 * half], F32, name="o", tag="o", bufs=6, align_bytes=64)
+            outs.append(o)
+        for e in range(2):
+            for c in range(C_TILES):
+                cols = slice(half * e, half * (e + 1))
+                if c % 2 == 1:
+                    nc.vector.tensor_scalar(
+                        out=outs[c][:, cols], in0=ends[(e, c)][:], scalar1=bias_bf[:, c, 0:1], scalar2=None, op0=ALU.add
+                    )
+                else:
+                    nc.scalar.activation(
+                        out=outs[c][:, cols], in_=ends[(e, c)][:], func=ACT.Identity, bias=bias_bf[:, c, 0:1]
+                    )
+                nc.sync.dma_start(
+                    out=out[P * c : P * (c + 1), n0 + half * e : n0 + half * (e + 1)], in_=outs[c][:, cols]
+                )

@@ -23,11 +23,9 @@ X_TILE = 512
 CHUNKS = [(0, 512), (512, 512), (1024, 512), (1536, 512)]
 F_TILES = FILTERS // P
 C_TILES = CHANNELS // P
-WARM = 36
 K0, RN, RD = 14, 1, 2
 VECTOR_UNITS = ((3,), 4)
 X_HEAD = 1024
-W_COLS = 128
 
 
 def tile_filter_bank_channel_mixer_s4_kernel(
@@ -64,9 +62,6 @@ def tile_filter_bank_channel_mixer_s4_kernel(
         gain_f = keep.tile([P, F_TILES], F32, name="gainf")
         sgn = keep.tile([P, F_TILES], F32, name="sgn")
         bias_bf = keep.tile([P, C_TILES, 2], BF16, name="biasbf")
-        warm = keep.tile([P, 4 * W_COLS], BF16, name="warm", align_bytes=64)
-        warm_c = keep.tile([P, W_COLS], U32, name="warmc", align_bytes=64)
-        warm_s = keep.tile([P, W_COLS], U8, name="warms", align_bytes=64)
         dummy = keep.tile([P, 1], F32, name="dummy")
 
         def load_bank(eng, h):
@@ -89,19 +84,6 @@ def tile_filter_bank_channel_mixer_s4_kernel(
 
         nc.gpsimd.memset(bs_raw[:].bitcast(I32), 0)
         nc.vector.memset(xs_head[:].bitcast(I32), 0)
-        nc.gpsimd.memset(warm[:].bitcast(U32), 0x3F803F80)
-        nc.vector.quantize_mx(out=warm_c[:].bitcast(FP8X4), scales=warm_s[:], in_=warm[:])
-        for u in range(WARM):
-            wz = psum.tile([P, W_COLS], F32, name="z", tag="z", bufs=4)
-            nc.tensor.matmul_mx(
-                out=wz[:],
-                lhsT=warm_c[:, 0:P].bitcast(FP8X4),
-                lhsT_scale=warm_s[:, 0:P],
-                rhs=warm_c[:].bitcast(FP8X4),
-                rhs_scale=warm_s[:],
-                start=True,
-                stop=True,
-            )
         nc.vector.memset(xs_rest[:].bitcast(I32), 0)
         nc.vector.memset(ms[:].bitcast(I32), 0)
         nc.vector.memset(dummy[:], 0.0)

@@ -9,6 +9,7 @@ F32 = mybir.dt.float32
 BF16 = mybir.dt.bfloat16
 I32 = mybir.dt.int32
 U32 = mybir.dt.uint32
+U16 = mybir.dt.uint16
 U8 = mybir.dt.uint8
 FP8X4 = mybir.dt.float8_e4m3fn_x4
 FP4X4 = mybir.dt.float4_e2m1fn_x4
@@ -19,19 +20,21 @@ P = 128
 PACK = 4
 K_PASS = P * PACK
 PASSES = 2
-X_TILE = 512
-CHUNKS = [(0, 512), (512, 512), (1024, 512), (1536, 512)]
-F_TILES = FILTERS // P
+WIDTHS = (512, 512, 512, 512)
 C_TILES = CHANNELS // P
-K0, RN, RD = 14, 1, 2
-VECTOR_UNITS = ((3,), 4)
-X_HEAD = 1024
+MIX_DELAY = 6
+MIX_EVERY = 3
+VECTOR_EVERY = 2
+INTERLEAVE_AT = 0
+QUANTIZE_AT = 2
+EMPTY_AT = 3
 
 
 def tile_filter_bank_channel_mixer_s4_kernel(
     tc, x_words, x_scales, bank_words, bank_scales, gain, mix_words, mix_scales, bias, out
 ):
     nc = tc.nc
+    starts = [sum(WIDTHS[:i]) for i in range(len(WIDTHS))]
     with ExitStack() as ctx:
         keep = ctx.enter_context(tc.tile_pool(name="keep", bufs=1))
         work = ctx.enter_context(tc.tile_pool(name="work", bufs=3))
@@ -40,285 +43,205 @@ def tile_filter_bank_channel_mixer_s4_kernel(
         ctx.enter_context(tc.manual_schedule())
 
         x_sb = []
-        for j in range(FRAMES // X_TILE):
-            xt = keep.tile([P, PASSES, 2 * X_TILE], U8, name="x%d" % j, align_bytes=64)
+        for i, w in enumerate(WIDTHS):
+            xt = keep.tile([P, PASSES, 2 * w], U8, name="x%d" % i, align_bytes=64)
             x_sb.append(xt)
-        b_raw = []
-        for h in range(2):
-            bt = keep.tile([P, PASSES, 2 * K_PASS], U8, name="braw%d" % h, align_bytes=64)
-            b_raw.append(bt)
-        b_sb, bs_sb = [], []
-        for f in range(F_TILES):
-            bt = keep.tile([P, PASSES, 2 * P], U8, name="b%d" % f, align_bytes=64)
-            b_sb.append(bt)
-            st = keep.tile([P, PASSES, P], U8, name="bs%d" % f, align_bytes=64)
-            bs_sb.append(st)
+        b_raw, bs_raw, b_sb, bs_sb = [], [], [], []
+        for h in range(PASSES):
+            raw = keep.tile([P, PASSES, 2 * K_PASS], U8, name="braw%d" % h, align_bytes=64)
+            b_raw.append(raw)
+            raw_scales = keep.tile([P, PASSES, K_PASS], U8, name="bsraw%d" % h, align_bytes=64)
+            bs_raw.append(raw_scales)
+            dealt = keep.tile([P, PACK, PASSES, 2 * P], U8, name="b%d" % h, align_bytes=64)
+            b_sb.append(dealt)
+            dealt_scales = keep.tile([P, PACK, PASSES, P], U8, name="bs%d" % h, align_bytes=64)
+            bs_sb.append(dealt_scales)
         m_sb = keep.tile([P, PASSES, 4 * CHANNELS], U8, name="mixw", align_bytes=64)
-        bs_raw = keep.tile([P, PASSES * FILTERS], U8, name="bsraw", align_bytes=64)
-        xs_head = keep.tile([P, PASSES * X_HEAD], U8, name="xshead", align_bytes=64)
-        xs_rest = keep.tile([P, PASSES * (FRAMES - X_HEAD)], U8, name="xsrest", align_bytes=64)
-        ms = keep.tile([P, PASSES * CHANNELS], U8, name="ms", align_bytes=64)
-        gain_bf = keep.tile([P, F_TILES], BF16, name="gainbf")
-        gain_f = keep.tile([P, F_TILES], F32, name="gainf")
-        sgn = keep.tile([P, F_TILES], F32, name="sgn")
+        xs_head = keep.tile([P, PASSES, WIDTHS[0]], U8, name="xshead", align_bytes=64)
+        xs_rest = keep.tile([P, PASSES, FRAMES - WIDTHS[0]], U8, name="xsrest", align_bytes=64)
+        ms = keep.tile([P, PASSES, CHANNELS], U8, name="ms", align_bytes=64)
+        gain_bf = keep.tile([P, PASSES, PACK], BF16, name="gainbf")
+        gain_f = keep.tile([P, PASSES, PACK], F32, name="gainf")
+        sgn = keep.tile([P, PASSES, PACK], F32, name="sgn")
         bias_bf = keep.tile([P, C_TILES, 2], BF16, name="biasbf")
-        dummy = keep.tile([P, 1], F32, name="dummy")
 
-        def load_bank(eng, h):
+        def clear(eng, tile):
+            eng.memset(tile[:].rearrange("p g n -> p (g n)").bitcast(I32), 0)
+
+        def load_words(eng, tile, src, first, count):
             eng.dma_start(
-                out=b_raw[h][:].bitcast(I32),
-                in_=bank_words[:, :, 2 * K_PASS * h : 2 * K_PASS * (h + 1)].rearrange("g p b -> p g b").bitcast(I32),
+                out=tile[:].bitcast(I32), in_=src[:, :, first : first + count].rearrange("g p b -> p g b").bitcast(I32)
             )
 
-        def load_x(eng, j):
-            eng.dma_start(
-                out=x_sb[j][:].bitcast(I32),
-                in_=x_words[:, :, 2 * X_TILE * j : 2 * X_TILE * (j + 1)].rearrange("g p b -> p g b").bitcast(I32),
-            )
+        def load_scales(eng, tile, src, first, count, rows):
+            for r in rows:
+                eng.dma_start(
+                    out=tile[r:P:32].bitcast(I32),
+                    in_=src[:, :, first : first + count].rearrange("g (q r) n -> r q g n", r=4)[r].bitcast(I32),
+                )
 
-        def load_scales(eng, tile, src, r):
-            eng.dma_start(
-                out=tile[r:P:32, :].rearrange("p (g n) -> p g n", g=PASSES).bitcast(I32),
-                in_=src.rearrange("g (q r) n -> r q g n", r=4)[r].bitcast(I32),
-            )
+        def load_x(eng, i):
+            load_words(eng, x_sb[i], x_words, 2 * starts[i], 2 * WIDTHS[i])
 
-        nc.gpsimd.memset(bs_raw[:].bitcast(I32), 0)
-        nc.vector.memset(xs_head[:].bitcast(I32), 0)
-        nc.vector.memset(xs_rest[:].bitcast(I32), 0)
-        nc.vector.memset(ms[:].bitcast(I32), 0)
-        nc.vector.memset(dummy[:], 0.0)
-        nc.scalar.activation(out=dummy[:], in_=dummy[:], func=ACT.Abs)
-
-        nc.sync.dma_start(
-            out=gain_bf[:].rearrange("p (h t) -> p h t", t=PACK), in_=gain.rearrange("(h p t) -> p h t", p=P, t=PACK)
-        )
-        for r in range(4):
-            load_scales(nc.sync, bs_raw, bank_scales, r)
-        load_bank(nc.sync, 0)
-        for r in range(1):
-            load_scales(nc.sync, xs_head, x_scales[:, :, 0:X_HEAD], r)
-        load_x(nc.sync, 0)
-        for r in range(1, 4):
-            load_scales(nc.sync, xs_head, x_scales[:, :, 0:X_HEAD], r)
-        load_bank(nc.sync, 1)
+        clear(nc.vector, bs_raw[0])
+        clear(nc.vector, xs_head)
+        load_scales(nc.sync, bs_raw[0], bank_scales, 0, K_PASS, range(2))
+        load_scales(nc.scalar, xs_head, x_scales, 0, WIDTHS[0], range(1))
+        load_scales(nc.sync, bs_raw[0], bank_scales, 0, K_PASS, range(2, 4))
+        load_words(nc.scalar, b_raw[0], bank_words, 0, 2 * K_PASS)
+        load_x(nc.scalar, 0)
+        nc.scalar.dma_start(out=gain_bf[:], in_=gain.rearrange("(h p t) -> p h t", p=P, t=PACK))
+        load_scales(nc.sync, xs_head, x_scales, 0, WIDTHS[0], range(1, 4))
+        clear(nc.vector, bs_raw[1])
+        clear(nc.vector, xs_rest)
+        clear(nc.vector, ms)
+        load_scales(nc.sync, bs_raw[1], bank_scales, K_PASS, K_PASS, range(2))
+        load_words(nc.sync, b_raw[1], bank_words, 2 * K_PASS, 2 * K_PASS)
+        load_scales(nc.sync, bs_raw[1], bank_scales, K_PASS, K_PASS, range(2, 4))
+        load_scales(nc.sync, xs_rest, x_scales, WIDTHS[0], FRAMES - WIDTHS[0], range(4))
         load_x(nc.sync, 1)
-        for r in range(4):
-            load_scales(nc.sync, ms, mix_scales, r)
-        for r in range(4):
-            load_scales(nc.sync, xs_rest, x_scales[:, :, X_HEAD:FRAMES], r)
+        load_scales(nc.sync, ms, mix_scales, 0, CHANNELS, range(4))
         nc.sync.dma_start(out=m_sb[:], in_=mix_words.rearrange("g p n t -> p g (n t)"))
-        nc.sync.dma_start(
-            out=bias_bf[:, :, 0:1], in_=bias.rearrange("(c p o) -> p c o", p=P, o=1)
-        )
-        load_x(nc.sync, 2)
-        load_x(nc.sync, 3)
+        nc.sync.dma_start(out=bias_bf[:, :, 0:1], in_=bias.rearrange("(c p o) -> p c o", p=P, o=1))
+        for i in range(2, len(WIDTHS)):
+            load_x(nc.sync, i)
 
-        def permute_codes(f):
-            h, t = divmod(f, PACK)
+        def deal(h, t0, t1):
             nc.vector.tensor_copy(
-                out=b_sb[f][:].rearrange("p g (m b) -> p g m b", b=2),
-                in_=b_raw[h][:].rearrange("p g (m t b) -> p t g m b", t=PACK, b=2)[:, t],
+                out=b_sb[h][:, t0:t1].bitcast(U16),
+                in_=b_raw[h][:].bitcast(U16).rearrange("p g (m t) -> p t g m", t=PACK)[:, t0:t1],
+            )
+            nc.vector.tensor_copy(
+                out=bs_sb[h][:, t0:t1], in_=bs_raw[h][:].rearrange("p g (m t) -> p t g m", t=PACK)[:, t0:t1]
             )
 
-        def permute_scales(f):
-            h, t = divmod(f, PACK)
-            nc.vector.tensor_copy(
-                out=bs_sb[f][:],
-                in_=bs_raw[:].rearrange("p (g h m t) -> p h t g m", g=PASSES, h=2, t=PACK)[:, h, t],
-            )
+        sub, grouped, codes = {}, {}, {}
 
-        sub = {}
-        ymap = {}
-        grouped = {}
-        codes = {}
-        zmap = {}
-
-        def x_scale_columns(g, n0, w):
-            if n0 < X_HEAD:
-                return xs_head[:, g * X_HEAD + n0 : g * X_HEAD + n0 + w]
-            start = g * (FRAMES - X_HEAD) + n0 - X_HEAD
-            return xs_rest[:, start : start + w]
-
-        def bank_pass(i, f):
-            n0, w = CHUNKS[i]
-            j, o = divmod(n0, X_TILE)
+        def filter_unit(i, h, t):
+            n0, w = starts[i], WIDTHS[i]
             y = psum.tile([P, w], F32, name="y", tag="y", bufs=4)
             for g in range(PASSES):
                 nc.tensor.matmul_mx(
                     out=y[:],
-                    lhsT=b_sb[f][:, g, :].bitcast(FP4X4),
-                    lhsT_scale=bs_sb[f][:, g, :],
-                    rhs=x_sb[j][:, g, 2 * o : 2 * (o + w)].bitcast(FP4X4),
-                    rhs_scale=x_scale_columns(g, n0, w),
+                    lhsT=b_sb[h][:, t, g, :].bitcast(FP4X4),
+                    lhsT_scale=bs_sb[h][:, t, g, :],
+                    rhs=x_sb[i][:, g, :].bitcast(FP4X4),
+                    rhs_scale=xs_head[:, g, :] if i == 0 else xs_rest[:, g, n0 - WIDTHS[0] : n0 - WIDTHS[0] + w],
                     start=(g == 0),
                     stop=(g == PASSES - 1),
                 )
-            ymap[(i, f)] = y
-
-        def rectify(i, f):
-            h, t = divmod(f, PACK)
-            w = CHUNKS[i][1]
             if t == 0:
                 s = work.tile([P, PACK, w], BF16, name="s", tag="s", bufs=4, align_bytes=64)
                 sub[(i, h)] = s
-            nc.scalar.activation(
-                out=sub[(i, h)][:, t, :], in_=ymap[(i, f)][:], func=ACT.Abs, scale=gain_f[:, f : f + 1]
-            )
+            nc.scalar.activation(out=sub[(i, h)][:, t, :], in_=y[:], func=ACT.Abs, scale=gain_f[:, h, t : t + 1])
 
-        def sign(i, f):
-            h, t = divmod(f, PACK)
-            nc.vector.tensor_scalar(
-                out=sub[(i, h)][:, t, :], in0=sub[(i, h)][:, t, :], scalar1=sgn[:, f : f + 1], scalar2=None, op0=ALU.mult
-            )
+        def sign(i, h, t):
+            rows = sub[(i, h)][:, t, :]
+            nc.vector.tensor_scalar(out=rows, in0=rows, scalar1=sgn[:, h, t : t + 1], scalar2=None, op0=ALU.mult)
 
-        def interleave(i, h):
-            w = CHUNKS[i][1]
+        def interleave(i, h, parts=1):
+            w = WIDTHS[i]
             gr = work.tile([P, w, PACK], BF16, name="gr", tag="gr", bufs=3, align_bytes=64)
-            nc.vector.tensor_copy(
-                out=gr[:].rearrange("p (c i) t -> p c t i", i=4), in_=sub[(i, h)][:].rearrange("p t (c i) -> p c t i", i=4)
-            )
+            for e in range(parts):
+                cols = slice(e * w // parts, (e + 1) * w // parts)
+                nc.vector.tensor_copy(
+                    out=gr[:, cols, :].rearrange("p (c i) t -> p c t i", i=4),
+                    in_=sub[(i, h)][:, :, cols].rearrange("p t (c i) -> p c t i", i=4),
+                )
             grouped[(i, h)] = gr
 
-        def quantize(i, h):
-            w = CHUNKS[i][1]
+        def quantize(i, h, parts=1):
+            w = WIDTHS[i]
             c = work.tile([P, w], U32, name="hc", tag="hc", bufs=6, align_bytes=64)
             sc = work.tile([P, w], U8, name="hs", tag="hs", bufs=6, align_bytes=64)
-            nc.vector.quantize_mx(
-                out=c[:].bitcast(FP8X4), scales=sc[:], in_=grouped[(i, h)][:].rearrange("p n t -> p (n t)")
-            )
+            for e in range(parts):
+                cols = slice(e * w // parts, (e + 1) * w // parts)
+                nc.vector.quantize_mx(
+                    out=c[:, cols].bitcast(FP8X4),
+                    scales=sc[:, cols],
+                    in_=grouped[(i, h)][:, cols, :].rearrange("p n t -> p (n t)"),
+                )
             codes[(i, h)] = (c, sc)
 
-        def mix_pass(i, c, g):
-            w = CHUNKS[i][1]
-            if g == 0:
-                z = psum.tile([P, w], F32, name="z", tag="z", bufs=4)
-                zmap[(i, c)] = z
+        def mix_pass(i, c, g, z, cols):
             hc, hs = codes[(i, g)]
             nc.tensor.matmul_mx(
-                out=zmap[(i, c)][:],
+                out=z[:],
                 lhsT=m_sb[:, g, 4 * P * c : 4 * P * (c + 1)].bitcast(FP8X4),
-                lhsT_scale=ms[:, g * CHANNELS + P * c : g * CHANNELS + P * (c + 1)],
-                rhs=hc[:].bitcast(FP8X4),
-                rhs_scale=hs[:],
+                lhsT_scale=ms[:, g, P * c : P * (c + 1)],
+                rhs=hc[:, cols].bitcast(FP8X4),
+                rhs_scale=hs[:, cols],
                 start=(g == 0),
                 stop=(g == PASSES - 1),
             )
 
-        def finish(i, c, on_vector):
-            n0, w = CHUNKS[i]
-            o = work.tile([P, w], F32, name="o", tag="o", bufs=6, align_bytes=64)
-            z = zmap[(i, c)]
+        def mix_unit(i, c, cols, tag="z"):
+            z = psum.tile([P, cols.stop - cols.start], F32, name=tag, tag=tag, bufs=4)
+            for g in range(PASSES):
+                mix_pass(i, c, g, z, cols)
+            return z
+
+        def finish(i, c, cols, z, on_vector):
+            n0, w = starts[i] + cols.start, cols.stop - cols.start
+            o = work.tile([P, w], F32, name="o", tag="o", bufs=8, align_bytes=64)
             if on_vector:
-                nc.vector.tensor_scalar(
-                    out=o[:], in0=z[:], scalar1=bias_bf[:, c, 0:1], scalar2=None, op0=ALU.add
-                )
+                nc.vector.tensor_scalar(out=o[:], in0=z[:], scalar1=bias_bf[:, c, 0:1], scalar2=None, op0=ALU.add)
             else:
                 nc.scalar.activation(out=o[:], in_=z[:], func=ACT.Identity, bias=bias_bf[:, c, 0:1])
             nc.sync.dma_start(out=out[P * c : P * (c + 1), n0 : n0 + w], in_=o[:])
 
-        for f in range(PACK):
-            permute_codes(f)
-            permute_scales(f)
-        nc.vector.tensor_copy(out=gain_f[:], in_=gain_bf[:])
-        nc.vector.tensor_scalar(out=sgn[:], in0=gain_f[:], scalar1=0.0, scalar2=2.0, op0=ALU.is_ge, op1=ALU.mult)
+        deal(0, 0, 1)
+        deal(0, 1, 2)
+        nc.scalar.activation(out=gain_f[:], in_=gain_bf[:], func=ACT.Abs)
+        nc.vector.tensor_scalar(out=sgn[:], in0=gain_bf[:], scalar1=0.0, scalar2=2.0, op0=ALU.is_ge, op1=ALU.mult)
+        deal(0, 2, PACK)
         nc.vector.tensor_scalar(out=sgn[:], in0=sgn[:], scalar1=-1.0, scalar2=None, op0=ALU.add)
+        deal(1, 0, 2)
 
-        order = [(i, f) for i in range(len(CHUNKS)) for f in range(F_TILES)]
-        last = len(CHUNKS) - 1
-        tasks = []
-        fresh = []
-        emitted = 0
-        for k, (i, f) in enumerate(order):
-            bank_pass(i, f)
-            rectify(i, f)
-            tasks += fresh
-            fresh = []
-            if k >= 1:
-                pi, pf = order[k - 1]
-                sign(pi, pf)
-                if pf % PACK == PACK - 1:
-                    fresh = [(interleave, (pi, pf // PACK)), (quantize, (pi, pf // PACK))]
-            if PACK + k < F_TILES:
-                permute_codes(PACK + k)
-                permute_scales(PACK + k)
-            for u in range(2 if len(tasks) > 2 else 1):
-                if tasks:
-                    what, args = tasks.pop(0)
-                    what(*args)
-            mi, c = divmod(emitted, C_TILES)
-            if (k - K0) * RN >= (emitted + 1) * RD and (mi, 1) in codes:
-                emitted += 1
-                for g in range(PASSES):
-                    mix_pass(mi, c, g)
-                if emitted % VECTOR_UNITS[1] in VECTOR_UNITS[0]:
-                    tasks.append((finish, (mi, c, True)))
-                else:
-                    finish(mi, c, False)
-        sign(last, F_TILES - 1)
-        for what, args in tasks:
-            what(*args)
-        half = CHUNKS[last][1] // 2
-        parts = []
-        for e in range(2):
-            gr = work.tile([P, half, PACK], BF16, name="gr", tag="gr", bufs=3, align_bytes=64)
-            nc.vector.tensor_copy(
-                out=gr[:].rearrange("p (c i) t -> p c t i", i=4),
-                in_=sub[(last, 1)][:, :, half * e : half * (e + 1)].rearrange("p t (c i) -> p c t i", i=4),
-            )
-            parts.append(gr)
-        tails = []
-        for e in range(2):
-            hc = work.tile([P, half], U32, name="hc", tag="hc", bufs=6, align_bytes=64)
-            hs = work.tile([P, half], U8, name="hs", tag="hs", bufs=6, align_bytes=64)
-            nc.vector.quantize_mx(
-                out=hc[:].bitcast(FP8X4), scales=hs[:], in_=parts[e][:].rearrange("p n t -> p (n t)")
-            )
-            tails.append((hc[:], hs[:]))
-        for u in range(emitted, last * C_TILES):
-            mi, c = divmod(u, C_TILES)
-            for g in range(PASSES):
-                mix_pass(mi, c, g)
-            finish(mi, c, False)
-        c0, s0 = codes[(last, 0)]
-        ends = {}
-        for g in range(PASSES):
-            for e in range(2):
-                if g == 0:
-                    hc, hs = c0[:, half * e : half * (e + 1)], s0[:, half * e : half * (e + 1)]
-                else:
-                    hc, hs = tails[e]
-                for c in range(C_TILES):
-                    if g == 0:
-                        if e == 0:
-                            z = psum.tile([P, half], F32, name="z", tag="z", bufs=4)
-                        else:
-                            z = psum.tile([P, half], F32, name="y", tag="y", bufs=4)
-                        ends[(e, c)] = z
-                    nc.tensor.matmul_mx(
-                        out=ends[(e, c)][:],
-                        lhsT=m_sb[:, g, 4 * P * c : 4 * P * (c + 1)].bitcast(FP8X4),
-                        lhsT_scale=ms[:, g * CHANNELS + P * c : g * CHANNELS + P * (c + 1)],
-                        rhs=hc.bitcast(FP8X4),
-                        rhs_scale=hs,
-                        start=(g == 0),
-                        stop=(g == PASSES - 1),
-                    )
-        n0 = CHUNKS[last][0]
-        outs = []
-        for c in range(C_TILES):
-            o = work.tile([P, 2 * half], F32, name="o", tag="o", bufs=6, align_bytes=64)
-            outs.append(o)
-        for e in range(2):
+        groups = [(i, h) for i in range(len(WIDTHS)) for h in range(PASSES)]
+        waiting = []
+        for_vector, held = [], []
+        step, last_mix, mixed = 0, -MIX_EVERY, 0
+        for n, (i, h) in enumerate(groups):
+            before = groups[n - 1] if n else None
+            for t in range(PACK):
+                filter_unit(i, h, t)
+                if waiting and waiting[0][0] <= step and step - last_mix >= MIX_EVERY:
+                    first, mi, c = waiting.pop(0)
+                    whole = slice(0, WIDTHS[mi])
+                    z = mix_unit(mi, c, whole)
+                    last_mix = step
+                    mixed += 1
+                    if n == len(groups) - 1 and t >= 2:
+                        held.append((mi, c, whole, z))
+                    elif mixed % VECTOR_EVERY == 0:
+                        for_vector.append((mi, c, whole, z))
+                    else:
+                        finish(mi, c, whole, z, False)
+                if t == 0 and before and INTERLEAVE_AT < 0:
+                    interleave(*before)
+                sign(i, h, t)
+                if n == 0 and t == 1:
+                    deal(1, 2, PACK)
+                if t == EMPTY_AT and for_vector:
+                    finish(*for_vector.pop(0), True)
+                if t == INTERLEAVE_AT and before:
+                    interleave(*before)
+                if t == QUANTIZE_AT and before:
+                    quantize(*before)
+                    if before[1] == PASSES - 1:
+                        waiting += [(step + MIX_DELAY, before[0], c) for c in range(C_TILES)]
+                step += 1
+        last = groups[-1]
+        interleave(*last, parts=2)
+        quantize(*last, parts=2)
+        for item in for_vector + held:
+            finish(*item, False)
+        for u, (first, mi, c) in enumerate(waiting):
+            whole = slice(0, WIDTHS[mi])
+            finish(mi, c, whole, mix_unit(mi, c, whole, "zy"[u % 2]), False)
+        part = WIDTHS[-1] // 1
+        for e in range(1):
             for c in range(C_TILES):
-                cols = slice(half * e, half * (e + 1))
-                if c % 2 == 1:
-                    nc.vector.tensor_scalar(
-                        out=outs[c][:, cols], in0=ends[(e, c)][:], scalar1=bias_bf[:, c, 0:1], scalar2=None, op0=ALU.add
-                    )
-                else:
-                    nc.scalar.activation(
-                        out=outs[c][:, cols], in_=ends[(e, c)][:], func=ACT.Identity, bias=bias_bf[:, c, 0:1]
-                    )
-                nc.sync.dma_start(
-                    out=out[P * c : P * (c + 1), n0 + half * e : n0 + half * (e + 1)], in_=outs[c][:, cols]
-                )
+                cols = slice(e * part, (e + 1) * part)
+                finish(last[0], c, cols, mix_unit(last[0], c, cols, "yz"[c % 2]), c % 2 == 0)

@@ -22,11 +22,12 @@ K_PASS = P * PACK
 PASSES = 2
 WIDTHS = (512, 512, 512, 512)
 C_TILES = CHANNELS // P
+WARM_COLS, WARM_PASSES = 256, 8
 MIX_DELAY = 6
-MIX_EVERY = 3
-VECTOR_EVERY = 2
+MIX_EVERY = 2
+VECTOR_EVERY = 3
 INTERLEAVE_AT = 0
-QUANTIZE_AT = 2
+QUANTIZE_AT = 3
 EMPTY_AT = 3
 
 
@@ -46,12 +47,11 @@ def tile_filter_bank_channel_mixer_s4_kernel(
         for i, w in enumerate(WIDTHS):
             xt = keep.tile([P, PASSES, 2 * w], U8, name="x%d" % i, align_bytes=64)
             x_sb.append(xt)
-        b_raw, bs_raw, b_sb, bs_sb = [], [], [], []
+        bs_raw = keep.tile([P, PASSES, FILTERS], U8, name="bsraw", align_bytes=64)
+        b_raw, b_sb, bs_sb = [], [], []
         for h in range(PASSES):
             raw = keep.tile([P, PASSES, 2 * K_PASS], U8, name="braw%d" % h, align_bytes=64)
             b_raw.append(raw)
-            raw_scales = keep.tile([P, PASSES, K_PASS], U8, name="bsraw%d" % h, align_bytes=64)
-            bs_raw.append(raw_scales)
             dealt = keep.tile([P, PACK, PASSES, 2 * P], U8, name="b%d" % h, align_bytes=64)
             b_sb.append(dealt)
             dealt_scales = keep.tile([P, PACK, PASSES, P], U8, name="bs%d" % h, align_bytes=64)
@@ -83,21 +83,36 @@ def tile_filter_bank_channel_mixer_s4_kernel(
         def load_x(eng, i):
             load_words(eng, x_sb[i], x_words, 2 * starts[i], 2 * WIDTHS[i])
 
-        clear(nc.vector, bs_raw[0])
+        clear(nc.vector, bs_raw)
         clear(nc.vector, xs_head)
-        load_scales(nc.sync, bs_raw[0], bank_scales, 0, K_PASS, range(2))
+        load_scales(nc.sync, bs_raw, bank_scales, 0, FILTERS, range(2))
         load_scales(nc.scalar, xs_head, x_scales, 0, WIDTHS[0], range(1))
-        load_scales(nc.sync, bs_raw[0], bank_scales, 0, K_PASS, range(2, 4))
+        load_scales(nc.sync, bs_raw, bank_scales, 0, FILTERS, range(2, 4))
         load_words(nc.scalar, b_raw[0], bank_words, 0, 2 * K_PASS)
         load_x(nc.scalar, 0)
         nc.scalar.dma_start(out=gain_bf[:], in_=gain.rearrange("(h p t) -> p h t", p=P, t=PACK))
         load_scales(nc.sync, xs_head, x_scales, 0, WIDTHS[0], range(1, 4))
-        clear(nc.vector, bs_raw[1])
+        load_words(nc.sync, b_raw[1], bank_words, 2 * K_PASS, 2 * K_PASS)
         clear(nc.vector, xs_rest)
         clear(nc.vector, ms)
-        load_scales(nc.sync, bs_raw[1], bank_scales, K_PASS, K_PASS, range(2))
-        load_words(nc.sync, b_raw[1], bank_words, 2 * K_PASS, 2 * K_PASS)
-        load_scales(nc.sync, bs_raw[1], bank_scales, K_PASS, K_PASS, range(2, 4))
+        warm_codes = keep.tile([P, WARM_COLS], U32, name="warmc", align_bytes=64)
+        warm_scales = keep.tile([P, WARM_COLS], U8, name="warms", align_bytes=64)
+        nc.vector.quantize_mx(
+            out=warm_codes[:].bitcast(FP8X4),
+            scales=warm_scales[:],
+            in_=xs_rest[:].rearrange("p g n -> p (g n)")[:, 0 : 2 * PACK * WARM_COLS].bitcast(BF16),
+        )
+        for u in range(WARM_PASSES):
+            unread = psum.tile([P, WARM_COLS], F32, name="z", tag="z", bufs=4)
+            nc.tensor.matmul_mx(
+                out=unread[:],
+                lhsT=warm_codes[:, 0:P].bitcast(FP8X4),
+                lhsT_scale=warm_scales[:, 0:P],
+                rhs=warm_codes[:].bitcast(FP8X4),
+                rhs_scale=warm_scales[:],
+                start=True,
+                stop=True,
+            )
         load_scales(nc.sync, xs_rest, x_scales, WIDTHS[0], FRAMES - WIDTHS[0], range(4))
         load_x(nc.sync, 1)
         load_scales(nc.sync, ms, mix_scales, 0, CHANNELS, range(4))
@@ -112,56 +127,62 @@ def tile_filter_bank_channel_mixer_s4_kernel(
                 in_=b_raw[h][:].bitcast(U16).rearrange("p g (m t) -> p t g m", t=PACK)[:, t0:t1],
             )
             nc.vector.tensor_copy(
-                out=bs_sb[h][:, t0:t1], in_=bs_raw[h][:].rearrange("p g (m t) -> p t g m", t=PACK)[:, t0:t1]
+                out=bs_sb[h][:, t0:t1],
+                in_=bs_raw[:].rearrange("p g (h m t) -> p h t g m", h=PASSES, t=PACK)[:, h, t0:t1],
             )
 
         sub, grouped, codes = {}, {}, {}
 
-        def filter_unit(i, h, t):
-            n0, w = starts[i], WIDTHS[i]
+        def filter_unit(group, t):
+            i, h, first, w = group
+            n0 = starts[i] + first
             y = psum.tile([P, w], F32, name="y", tag="y", bufs=4)
             for g in range(PASSES):
                 nc.tensor.matmul_mx(
                     out=y[:],
                     lhsT=b_sb[h][:, t, g, :].bitcast(FP4X4),
                     lhsT_scale=bs_sb[h][:, t, g, :],
-                    rhs=x_sb[i][:, g, :].bitcast(FP4X4),
-                    rhs_scale=xs_head[:, g, :] if i == 0 else xs_rest[:, g, n0 - WIDTHS[0] : n0 - WIDTHS[0] + w],
+                    rhs=x_sb[i][:, g, 2 * first : 2 * (first + w)].bitcast(FP4X4),
+                    rhs_scale=xs_head[:, g, n0 : n0 + w] if i == 0 else xs_rest[:, g, n0 - WIDTHS[0] : n0 - WIDTHS[0] + w],
                     start=(g == 0),
                     stop=(g == PASSES - 1),
                 )
             if t == 0:
-                s = work.tile([P, PACK, w], BF16, name="s", tag="s", bufs=4, align_bytes=64)
-                sub[(i, h)] = s
-            nc.scalar.activation(out=sub[(i, h)][:, t, :], in_=y[:], func=ACT.Abs, scale=gain_f[:, h, t : t + 1])
+                s = work.tile([P, PACK, w], BF16, name="s", tag="s", bufs=10, align_bytes=64)
+                sub[group] = s
+            nc.scalar.activation(out=sub[group][:, t, :], in_=y[:], func=ACT.Abs, scale=gain_f[:, h, t : t + 1])
 
-        def sign(i, h, t):
-            rows = sub[(i, h)][:, t, :]
-            nc.vector.tensor_scalar(out=rows, in0=rows, scalar1=sgn[:, h, t : t + 1], scalar2=None, op0=ALU.mult)
+        def sign(group, t):
+            rows = sub[group][:, t, :]
+            nc.vector.tensor_scalar(
+                out=rows, in0=rows, scalar1=sgn[:, group[1], t : t + 1], scalar2=None, op0=ALU.mult
+            )
 
-        def interleave(i, h, parts=1):
-            w = WIDTHS[i]
-            gr = work.tile([P, w, PACK], BF16, name="gr", tag="gr", bufs=3, align_bytes=64)
+        def interleave(group, parts=1):
+            w = group[3]
+            gr = work.tile([P, w, PACK], BF16, name="gr", tag="gr", bufs=10, align_bytes=64)
             for e in range(parts):
                 cols = slice(e * w // parts, (e + 1) * w // parts)
                 nc.vector.tensor_copy(
                     out=gr[:, cols, :].rearrange("p (c i) t -> p c t i", i=4),
-                    in_=sub[(i, h)][:, :, cols].rearrange("p t (c i) -> p c t i", i=4),
+                    in_=sub[group][:, :, cols].rearrange("p t (c i) -> p c t i", i=4),
                 )
-            grouped[(i, h)] = gr
+            grouped[group] = gr
 
-        def quantize(i, h, parts=1):
-            w = WIDTHS[i]
-            c = work.tile([P, w], U32, name="hc", tag="hc", bufs=6, align_bytes=64)
-            sc = work.tile([P, w], U8, name="hs", tag="hs", bufs=6, align_bytes=64)
+        def quantize(group, parts=1):
+            i, h, first, w = group
+            if first == 0:
+                c = work.tile([P, WIDTHS[i]], U32, name="hc", tag="hc", bufs=8, align_bytes=64)
+                sc = work.tile([P, WIDTHS[i]], U8, name="hs", tag="hs", bufs=8, align_bytes=64)
+                codes[(i, h)] = (c, sc)
+            c, sc = codes[(i, h)]
             for e in range(parts):
-                cols = slice(e * w // parts, (e + 1) * w // parts)
+                lo, hi = e * w // parts, (e + 1) * w // parts
                 nc.vector.quantize_mx(
-                    out=c[:, cols].bitcast(FP8X4),
-                    scales=sc[:, cols],
-                    in_=grouped[(i, h)][:, cols, :].rearrange("p n t -> p (n t)"),
+                    out=c[:, first + lo : first + hi].bitcast(FP8X4),
+                    scales=sc[:, first + lo : first + hi],
+                    in_=grouped[group][:, lo:hi, :].rearrange("p n t -> p (n t)"),
                 )
-            codes[(i, h)] = (c, sc)
 
         def mix_pass(i, c, g, z, cols):
             hc, hs = codes[(i, g)]
@@ -183,7 +204,7 @@ def tile_filter_bank_channel_mixer_s4_kernel(
 
         def finish(i, c, cols, z, on_vector):
             n0, w = starts[i] + cols.start, cols.stop - cols.start
-            o = work.tile([P, w], F32, name="o", tag="o", bufs=8, align_bytes=64)
+            o = work.tile([P, w], F32, name="o", tag="o", bufs=20, align_bytes=64)
             if on_vector:
                 nc.vector.tensor_scalar(out=o[:], in0=z[:], scalar1=bias_bf[:, c, 0:1], scalar2=None, op0=ALU.add)
             else:
@@ -191,57 +212,53 @@ def tile_filter_bank_channel_mixer_s4_kernel(
             nc.sync.dma_start(out=out[P * c : P * (c + 1), n0 : n0 + w], in_=o[:])
 
         deal(0, 0, 1)
-        deal(0, 1, 2)
+        deal(0, 1, PACK)
         nc.scalar.activation(out=gain_f[:], in_=gain_bf[:], func=ACT.Abs)
-        nc.vector.tensor_scalar(out=sgn[:], in0=gain_bf[:], scalar1=0.0, scalar2=2.0, op0=ALU.is_ge, op1=ALU.mult)
-        deal(0, 2, PACK)
-        nc.vector.tensor_scalar(out=sgn[:], in0=sgn[:], scalar1=-1.0, scalar2=None, op0=ALU.add)
-        deal(1, 0, 2)
+        nc.scalar.activation(out=sgn[:], in_=gain_bf[:], func=ACT.Sign)
+        deal(1, 0, PACK)
 
-        groups = [(i, h) for i in range(len(WIDTHS)) for h in range(PASSES)]
+        groups = [(i, h, 0, w) for i, w in enumerate(WIDTHS) for h in range(PASSES)]
+        for at, cuts in ((len(groups) - 1, (256, 256)), (0, (512,))):
+            i, h, first, w = groups[at]
+            groups[at : at + 1] = [(i, h, sum(cuts[:e]), cuts[e]) for e in range(len(cuts))]
         waiting = []
         for_vector, held = [], []
         step, last_mix, mixed = 0, -MIX_EVERY, 0
-        for n, (i, h) in enumerate(groups):
+        for n, group in enumerate(groups):
             before = groups[n - 1] if n else None
             for t in range(PACK):
-                filter_unit(i, h, t)
-                if waiting and waiting[0][0] <= step and step - last_mix >= MIX_EVERY:
-                    first, mi, c = waiting.pop(0)
-                    whole = slice(0, WIDTHS[mi])
-                    z = mix_unit(mi, c, whole)
+                filter_unit(group, t)
+                if waiting and waiting[0][0] <= step and step - last_mix >= MIX_EVERY and step < 99:
+                    first, mi, c, cols = waiting.pop(0)
+                    z = mix_unit(mi, c, cols)
                     last_mix = step
                     mixed += 1
-                    if n == len(groups) - 1 and t >= 2:
-                        held.append((mi, c, whole, z))
-                    elif mixed % VECTOR_EVERY == 0:
-                        for_vector.append((mi, c, whole, z))
+                    if n == len(groups) - 1 and t >= 4:
+                        held.append((mi, c, cols, z))
+                    elif mixed % VECTOR_EVERY == 0 and mixed <= 6:
+                        for_vector.append((mi, c, cols, z))
                     else:
-                        finish(mi, c, whole, z, False)
-                if t == 0 and before and INTERLEAVE_AT < 0:
-                    interleave(*before)
-                sign(i, h, t)
-                if n == 0 and t == 1:
-                    deal(1, 2, PACK)
+                        finish(mi, c, cols, z, False)
+                if t == 0 and before and (INTERLEAVE_AT < 0 or n <= 1):
+                    interleave(before)
+                sign(group, t)
                 if t == EMPTY_AT and for_vector:
                     finish(*for_vector.pop(0), True)
-                if t == INTERLEAVE_AT and before:
-                    interleave(*before)
+                if t == INTERLEAVE_AT and before and n > 1:
+                    interleave(before)
                 if t == QUANTIZE_AT and before:
-                    quantize(*before)
+                    quantize(before)
                     if before[1] == PASSES - 1:
-                        waiting += [(step + MIX_DELAY, before[0], c) for c in range(C_TILES)]
+                        cols = slice(before[2], before[2] + before[3])
+                        waiting += [(step + MIX_DELAY + 0 * before[0], before[0], c, cols) for c in range(C_TILES)]
                 step += 1
         last = groups[-1]
-        interleave(*last, parts=2)
-        quantize(*last, parts=2)
+        interleave(last, parts=2)
+        quantize(last, parts=2)
         for item in for_vector + held:
             finish(*item, False)
-        for u, (first, mi, c) in enumerate(waiting):
-            whole = slice(0, WIDTHS[mi])
-            finish(mi, c, whole, mix_unit(mi, c, whole, "zy"[u % 2]), False)
-        part = WIDTHS[-1] // 1
-        for e in range(1):
-            for c in range(C_TILES):
-                cols = slice(e * part, (e + 1) * part)
-                finish(last[0], c, cols, mix_unit(last[0], c, cols, "yz"[c % 2]), c % 2 == 0)
+        cols = slice(last[2], last[2] + last[3])
+        waiting += [(step, last[0], c, cols) for c in range(C_TILES)]
+        for u, (first, mi, c, cols) in enumerate(waiting):
+            on_vector = u >= len(waiting) - 4 and u % 2 == 0
+            finish(mi, c, cols, mix_unit(mi, c, cols, "zy"[u % 2]), on_vector)

@@ -22,7 +22,7 @@ K_PASS = P * PACK
 PASSES = 2
 WIDTHS = (512, 512, 512, 512)
 C_TILES = CHANNELS // P
-WARM_COLS, WARM_PASSES = 256, 8
+WARM_PASSES = 3
 MIX_DELAY = 6
 MIX_EVERY = 2
 VECTOR_EVERY = 3
@@ -85,34 +85,15 @@ def tile_filter_bank_channel_mixer_s4_kernel(
 
         clear(nc.vector, bs_raw)
         clear(nc.vector, xs_head)
-        load_scales(nc.sync, bs_raw, bank_scales, 0, FILTERS, range(2))
+        load_scales(nc.sync, bs_raw, bank_scales, 0, FILTERS, range(4))
         load_scales(nc.scalar, xs_head, x_scales, 0, WIDTHS[0], range(1))
-        load_scales(nc.sync, bs_raw, bank_scales, 0, FILTERS, range(2, 4))
         load_words(nc.scalar, b_raw[0], bank_words, 0, 2 * K_PASS)
         load_x(nc.scalar, 0)
-        nc.scalar.dma_start(out=gain_bf[:], in_=gain.rearrange("(h p t) -> p h t", p=P, t=PACK))
+        load_words(nc.scalar, b_raw[1], bank_words, 2 * K_PASS, 2 * K_PASS)
         load_scales(nc.sync, xs_head, x_scales, 0, WIDTHS[0], range(1, 4))
-        load_words(nc.sync, b_raw[1], bank_words, 2 * K_PASS, 2 * K_PASS)
+        nc.sync.dma_start(out=gain_bf[:], in_=gain.rearrange("(h p t) -> p h t", p=P, t=PACK))
         clear(nc.vector, xs_rest)
         clear(nc.vector, ms)
-        warm_codes = keep.tile([P, WARM_COLS], U32, name="warmc", align_bytes=64)
-        warm_scales = keep.tile([P, WARM_COLS], U8, name="warms", align_bytes=64)
-        nc.vector.quantize_mx(
-            out=warm_codes[:].bitcast(FP8X4),
-            scales=warm_scales[:],
-            in_=xs_rest[:].rearrange("p g n -> p (g n)")[:, 0 : 2 * PACK * WARM_COLS].bitcast(BF16),
-        )
-        for u in range(WARM_PASSES):
-            unread = psum.tile([P, WARM_COLS], F32, name="z", tag="z", bufs=4)
-            nc.tensor.matmul_mx(
-                out=unread[:],
-                lhsT=warm_codes[:, 0:P].bitcast(FP8X4),
-                lhsT_scale=warm_scales[:, 0:P],
-                rhs=warm_codes[:].bitcast(FP8X4),
-                rhs_scale=warm_scales[:],
-                start=True,
-                stop=True,
-            )
         load_scales(nc.sync, xs_rest, x_scales, WIDTHS[0], FRAMES - WIDTHS[0], range(4))
         load_x(nc.sync, 1)
         load_scales(nc.sync, ms, mix_scales, 0, CHANNELS, range(4))
@@ -120,6 +101,18 @@ def tile_filter_bank_channel_mixer_s4_kernel(
         nc.sync.dma_start(out=bias_bf[:, :, 0:1], in_=bias.rearrange("(c p o) -> p c o", p=P, o=1))
         for i in range(2, len(WIDTHS)):
             load_x(nc.sync, i)
+        for u in range(WARM_PASSES):
+            unread = psum.tile([P, K_PASS], F32, name="z", tag="z", bufs=4)
+            nc.tensor.matmul_mx(
+                out=unread[:],
+                lhsT=bs_raw[:, 1, 0 : 2 * P].bitcast(FP4X4),
+                lhsT_scale=bs_raw[:, 0, 0:P],
+                rhs=bs_raw[:, 1, :].bitcast(FP4X4),
+                rhs_scale=bs_raw[:, 0, 0:K_PASS],
+                start=True,
+                stop=True,
+            )
+
 
         def deal(h, t0, t1):
             nc.vector.tensor_copy(
@@ -213,9 +206,9 @@ def tile_filter_bank_channel_mixer_s4_kernel(
 
         deal(0, 0, 1)
         deal(0, 1, PACK)
+        deal(1, 0, PACK)
         nc.scalar.activation(out=gain_f[:], in_=gain_bf[:], func=ACT.Abs)
         nc.scalar.activation(out=sgn[:], in_=gain_bf[:], func=ACT.Sign)
-        deal(1, 0, PACK)
 
         groups = [(i, h, 0, w) for i, w in enumerate(WIDTHS) for h in range(PASSES)]
         for at, cuts in ((len(groups) - 1, (256, 256)), (0, (512,))):

@@ -22,7 +22,8 @@ K_PASS = P * PACK
 PASSES = 2
 WIDTHS = (512, 512, 512, 512)
 C_TILES = CHANNELS // P
-WARM_PASSES = 3
+WARM_PASSES = 0
+EARLY_QUADRANTS = (0, 2, 1)
 MIX_DELAY = 6
 MIX_EVERY = 2
 VECTOR_EVERY = 3
@@ -83,17 +84,33 @@ def tile_filter_bank_channel_mixer_s4_kernel(
         def load_x(eng, i):
             load_words(eng, x_sb[i], x_words, 2 * starts[i], 2 * WIDTHS[i])
 
+        def load_quadrant(eng, tile, src, first, count, q):
+            eng.dma_start(
+                out=tile[32 * q : 32 * q + 4].bitcast(I32),
+                in_=src[:, 4 * q : 4 * q + 4, first : first + count].rearrange("g r n -> r g n").bitcast(I32),
+            )
+
+        bs_early = keep.tile([P, PASSES, FILTERS], U8, name="bsearly", align_bytes=64)
+        for q, eng in zip(EARLY_QUADRANTS, (nc.sync, nc.scalar, nc.sync)):
+            load_quadrant(eng, bs_early, bank_scales, 0, FILTERS, q)
+        load_words(nc.scalar, b_raw[0], bank_words, 0, 2 * K_PASS)
+        load_x(nc.sync, 0)
         clear(nc.vector, bs_raw)
         clear(nc.vector, xs_head)
-        load_scales(nc.sync, bs_raw, bank_scales, 0, FILTERS, range(4))
-        load_scales(nc.scalar, xs_head, x_scales, 0, WIDTHS[0], range(1))
-        load_words(nc.scalar, b_raw[0], bank_words, 0, 2 * K_PASS)
-        load_x(nc.scalar, 0)
-        load_words(nc.scalar, b_raw[1], bank_words, 2 * K_PASS, 2 * K_PASS)
-        load_scales(nc.sync, xs_head, x_scales, 0, WIDTHS[0], range(1, 4))
-        nc.sync.dma_start(out=gain_bf[:], in_=gain.rearrange("(h p t) -> p h t", p=P, t=PACK))
+        load_quadrant(nc.scalar, bs_raw, bank_scales, 0, FILTERS, 3)
+        load_quadrant(nc.sync, xs_head, x_scales, 0, WIDTHS[0], 0)
+        nc.scalar.dma_start(out=gain_bf[:], in_=gain.rearrange("(h p t) -> p h t", p=P, t=PACK))
+        for q, eng in zip((1, 2, 3), (nc.sync, nc.scalar, nc.sync)):
+            load_quadrant(eng, xs_head, x_scales, 0, WIDTHS[0], q)
+        load_words(nc.sync, b_raw[1], bank_words, 2 * K_PASS, 2 * K_PASS)
         clear(nc.vector, xs_rest)
         clear(nc.vector, ms)
+        for q in EARLY_QUADRANTS:
+            rows = slice(32 * q, 32 * q + 4)
+            nc.vector.tensor_copy(
+                out=bs_raw[rows].rearrange("p g n -> p (g n)").bitcast(I32),
+                in_=bs_early[rows].rearrange("p g n -> p (g n)").bitcast(I32),
+            )
         load_scales(nc.sync, xs_rest, x_scales, WIDTHS[0], FRAMES - WIDTHS[0], range(4))
         load_x(nc.sync, 1)
         load_scales(nc.sync, ms, mix_scales, 0, CHANNELS, range(4))
@@ -206,7 +223,8 @@ def tile_filter_bank_channel_mixer_s4_kernel(
 
         deal(0, 0, 1)
         deal(0, 1, PACK)
-        deal(1, 0, PACK)
+        deal(1, 0, 2)
+        deal(1, 2, PACK)
         nc.scalar.activation(out=gain_f[:], in_=gain_bf[:], func=ACT.Abs)
         nc.scalar.activation(out=sgn[:], in_=gain_bf[:], func=ACT.Sign)
 
@@ -239,7 +257,7 @@ def tile_filter_bank_channel_mixer_s4_kernel(
                     finish(*for_vector.pop(0), True)
                 if t == INTERLEAVE_AT and before and n > 1:
                     interleave(before)
-                if t == QUANTIZE_AT and before:
+                if t == (QUANTIZE_AT if n < len(groups) - 1 else 2) and before:
                     quantize(before)
                     if before[1] == PASSES - 1:
                         cols = slice(before[2], before[2] + before[3])
@@ -252,6 +270,16 @@ def tile_filter_bank_channel_mixer_s4_kernel(
             finish(*item, False)
         cols = slice(last[2], last[2] + last[3])
         waiting += [(step, last[0], c, cols) for c in range(C_TILES)]
-        for u, (first, mi, c, cols) in enumerate(waiting):
-            on_vector = u >= len(waiting) - 4 and u % 2 == 0
-            finish(mi, c, cols, mix_unit(mi, c, cols, "zy"[u % 2]), on_vector)
+        for first, mi, c, cols in [u for u in waiting if u[1] < last[0]]:
+            finish(mi, c, cols, mix_unit(mi, c, cols), False)
+        ending = [u for u in waiting if u[1] == last[0]]
+        for e in range(0, len(ending), C_TILES):
+            banks = []
+            for first, mi, c, cols in ending[e : e + C_TILES]:
+                tag = "y" if e == 0 else "z"
+                z = psum.tile([P, cols.stop - cols.start], F32, name=tag, tag=tag, bufs=4)
+                mix_pass(mi, c, 0, z, cols)
+                banks.append(z)
+            for (first, mi, c, cols), z in zip(ending[e : e + C_TILES], banks):
+                mix_pass(mi, c, 1, z, cols)
+                finish(mi, c, cols, z, e + C_TILES >= len(ending) and c % 2 == 0)

@@ -22,11 +22,11 @@ K_PASS = P * PACK
 PASSES = 2
 WIDTHS = (512, 512, 512, 512)
 C_TILES = CHANNELS // P
-WARM_PASSES = 0
+WARM_PASSES = 3
 EARLY_QUADRANTS = (0, 2, 1)
 MIX_DELAY = 6
 MIX_EVERY = 2
-VECTOR_EVERY = 3
+VECTOR_EVERY = 2
 INTERLEAVE_AT = 0
 QUANTIZE_AT = 3
 EMPTY_AT = 3
@@ -93,15 +93,14 @@ def tile_filter_bank_channel_mixer_s4_kernel(
         bs_early = keep.tile([P, PASSES, FILTERS], U8, name="bsearly", align_bytes=64)
         for q, eng in zip(EARLY_QUADRANTS, (nc.sync, nc.scalar, nc.sync)):
             load_quadrant(eng, bs_early, bank_scales, 0, FILTERS, q)
-        load_words(nc.scalar, b_raw[0], bank_words, 0, 2 * K_PASS)
-        load_x(nc.sync, 0)
         clear(nc.vector, bs_raw)
         clear(nc.vector, xs_head)
         load_quadrant(nc.scalar, bs_raw, bank_scales, 0, FILTERS, 3)
-        load_quadrant(nc.sync, xs_head, x_scales, 0, WIDTHS[0], 0)
+        load_scales(nc.sync, xs_head, x_scales, 0, WIDTHS[0], range(1))
+        load_words(nc.scalar, b_raw[0], bank_words, 0, 2 * K_PASS)
+        load_x(nc.scalar, 0)
         nc.scalar.dma_start(out=gain_bf[:], in_=gain.rearrange("(h p t) -> p h t", p=P, t=PACK))
-        for q, eng in zip((1, 2, 3), (nc.sync, nc.scalar, nc.sync)):
-            load_quadrant(eng, xs_head, x_scales, 0, WIDTHS[0], q)
+        load_scales(nc.sync, xs_head, x_scales, 0, WIDTHS[0], range(1, 4))
         load_words(nc.sync, b_raw[1], bank_words, 2 * K_PASS, 2 * K_PASS)
         clear(nc.vector, xs_rest)
         clear(nc.vector, ms)
@@ -257,7 +256,7 @@ def tile_filter_bank_channel_mixer_s4_kernel(
                     finish(*for_vector.pop(0), True)
                 if t == INTERLEAVE_AT and before and n > 1:
                     interleave(before)
-                if t == (QUANTIZE_AT if n < len(groups) - 1 else 2) and before:
+                if t == (QUANTIZE_AT if n < len(groups) - 1 else 3) and before:
                     quantize(before)
                     if before[1] == PASSES - 1:
                         cols = slice(before[2], before[2] + before[3])

@@ -22,11 +22,11 @@ K_PASS = P * PACK
 PASSES = 2
 WIDTHS = (512, 512, 512, 512)
 C_TILES = CHANNELS // P
-WARM_PASSES = 3
-EARLY_QUADRANTS = (0, 2, 1)
+WARM_COLS, EARLY_WARM, WARM_PASSES = 256, 6, 2
+EARLY_QUADRANTS = (0, 2, 1, 3)
 MIX_DELAY = 6
 MIX_EVERY = 2
-VECTOR_EVERY = 2
+VECTOR_EVERY = 3
 INTERLEAVE_AT = 0
 QUANTIZE_AT = 3
 EMPTY_AT = 3
@@ -59,8 +59,9 @@ def tile_filter_bank_channel_mixer_s4_kernel(
             bs_sb.append(dealt_scales)
         m_sb = keep.tile([P, PASSES, 4 * CHANNELS], U8, name="mixw", align_bytes=64)
         xs_head = keep.tile([P, PASSES, WIDTHS[0]], U8, name="xshead", align_bytes=64)
-        xs_rest = keep.tile([P, PASSES, FRAMES - WIDTHS[0]], U8, name="xsrest", align_bytes=64)
-        ms = keep.tile([P, PASSES, CHANNELS], U8, name="ms", align_bytes=64)
+        late = keep.tile([P, PASSES * (FRAMES - WIDTHS[0] + CHANNELS)], U8, name="late", align_bytes=64)
+        xs_rest = late[:, 0 : PASSES * (FRAMES - WIDTHS[0])].rearrange("p (g n) -> p g n", g=PASSES)
+        ms = late[:, PASSES * (FRAMES - WIDTHS[0]) :].rearrange("p (g n) -> p g n", g=PASSES)
         gain_bf = keep.tile([P, PASSES, PACK], BF16, name="gainbf")
         gain_f = keep.tile([P, PASSES, PACK], F32, name="gainf")
         sgn = keep.tile([P, PASSES, PACK], F32, name="sgn")
@@ -91,25 +92,41 @@ def tile_filter_bank_channel_mixer_s4_kernel(
             )
 
         bs_early = keep.tile([P, PASSES, FILTERS], U8, name="bsearly", align_bytes=64)
-        for q, eng in zip(EARLY_QUADRANTS, (nc.sync, nc.scalar, nc.sync)):
+        for q, eng in zip(EARLY_QUADRANTS, (nc.sync, nc.scalar, nc.sync, nc.scalar)):
             load_quadrant(eng, bs_early, bank_scales, 0, FILTERS, q)
-        clear(nc.vector, bs_raw)
         clear(nc.vector, xs_head)
-        load_quadrant(nc.scalar, bs_raw, bank_scales, 0, FILTERS, 3)
-        load_scales(nc.sync, xs_head, x_scales, 0, WIDTHS[0], range(1))
+        clear(nc.vector, bs_raw)
+        load_scales(nc.scalar, xs_head, x_scales, 0, WIDTHS[0], range(1))
         load_words(nc.scalar, b_raw[0], bank_words, 0, 2 * K_PASS)
         load_x(nc.scalar, 0)
         nc.scalar.dma_start(out=gain_bf[:], in_=gain.rearrange("(h p t) -> p h t", p=P, t=PACK))
         load_scales(nc.sync, xs_head, x_scales, 0, WIDTHS[0], range(1, 4))
         load_words(nc.sync, b_raw[1], bank_words, 2 * K_PASS, 2 * K_PASS)
-        clear(nc.vector, xs_rest)
-        clear(nc.vector, ms)
-        for q in EARLY_QUADRANTS:
-            rows = slice(32 * q, 32 * q + 4)
-            nc.vector.tensor_copy(
-                out=bs_raw[rows].rearrange("p g n -> p (g n)").bitcast(I32),
-                in_=bs_early[rows].rearrange("p g n -> p (g n)").bitcast(I32),
+        warm_codes = keep.tile([P, WARM_COLS], U32, name="warmc", align_bytes=64)
+        warm_scales = keep.tile([P, WARM_COLS], U8, name="warms", align_bytes=64)
+        nc.vector.quantize_mx(
+            out=warm_codes[:].bitcast(FP8X4),
+            scales=warm_scales[:],
+            in_=bs_raw[:].rearrange("p g n -> p (g n)").bitcast(BF16),
+        )
+        for u in range(EARLY_WARM):
+            unread = psum.tile([P, WARM_COLS], F32, name="z", tag="z", bufs=4)
+            nc.tensor.matmul_mx(
+                out=unread[:],
+                lhsT=warm_codes[:, 0:P].bitcast(FP8X4),
+                lhsT_scale=warm_scales[:, 0:P],
+                rhs=warm_codes[:].bitcast(FP8X4),
+                rhs_scale=warm_scales[:],
+                start=True,
+                stop=True,
             )
+        nc.vector.memset(late[:].bitcast(I32), 0)
+        def settle(h):
+            for q in EARLY_QUADRANTS:
+                rows, cols = slice(32 * q, 32 * q + 4), slice(K_PASS * h, K_PASS * (h + 1))
+                nc.vector.tensor_copy(out=bs_raw[rows, :, cols].bitcast(I32), in_=bs_early[rows, :, cols].bitcast(I32))
+
+        settle(0)
         load_scales(nc.sync, xs_rest, x_scales, WIDTHS[0], FRAMES - WIDTHS[0], range(4))
         load_x(nc.sync, 1)
         load_scales(nc.sync, ms, mix_scales, 0, CHANNELS, range(4))
@@ -121,9 +138,9 @@ def tile_filter_bank_channel_mixer_s4_kernel(
             unread = psum.tile([P, K_PASS], F32, name="z", tag="z", bufs=4)
             nc.tensor.matmul_mx(
                 out=unread[:],
-                lhsT=bs_raw[:, 1, 0 : 2 * P].bitcast(FP4X4),
+                lhsT=b_raw[0][:, 0, 0 : 2 * P].bitcast(FP4X4),
                 lhsT_scale=bs_raw[:, 0, 0:P],
-                rhs=bs_raw[:, 1, :].bitcast(FP4X4),
+                rhs=b_raw[0][:, 0, :].bitcast(FP4X4),
                 rhs_scale=bs_raw[:, 0, 0:K_PASS],
                 start=True,
                 stop=True,
@@ -221,7 +238,9 @@ def tile_filter_bank_channel_mixer_s4_kernel(
             nc.sync.dma_start(out=out[P * c : P * (c + 1), n0 : n0 + w], in_=o[:])
 
         deal(0, 0, 1)
-        deal(0, 1, PACK)
+        deal(0, 1, 2)
+        deal(0, 2, PACK)
+        settle(1)
         deal(1, 0, 2)
         deal(1, 2, PACK)
         nc.scalar.activation(out=gain_f[:], in_=gain_bf[:], func=ACT.Abs)
@@ -238,7 +257,7 @@ def tile_filter_bank_channel_mixer_s4_kernel(
             before = groups[n - 1] if n else None
             for t in range(PACK):
                 filter_unit(group, t)
-                if waiting and waiting[0][0] <= step and step - last_mix >= MIX_EVERY and step < 99:
+                if waiting and waiting[0][0] <= step and step - last_mix >= (MIX_EVERY if step < 32 else 1) and step < 99:
                     first, mi, c, cols = waiting.pop(0)
                     z = mix_unit(mi, c, cols)
                     last_mix = step

@@ -22,7 +22,6 @@ K_PASS = P * PACK
 PASSES = 2
 WIDTHS = (512, 512, 512, 512)
 C_TILES = CHANNELS // P
-WARM_COLS, EARLY_WARM, WARM_PASSES = 256, 6, 2
 EARLY_QUADRANTS = (0, 2, 1, 3)
 MIX_DELAY = 6
 MIX_EVERY = 2
@@ -102,24 +101,6 @@ def tile_filter_bank_channel_mixer_s4_kernel(
         nc.scalar.dma_start(out=gain_bf[:], in_=gain.rearrange("(h p t) -> p h t", p=P, t=PACK))
         load_scales(nc.sync, xs_head, x_scales, 0, WIDTHS[0], range(1, 4))
         load_words(nc.sync, b_raw[1], bank_words, 2 * K_PASS, 2 * K_PASS)
-        warm_codes = keep.tile([P, WARM_COLS], U32, name="warmc", align_bytes=64)
-        warm_scales = keep.tile([P, WARM_COLS], U8, name="warms", align_bytes=64)
-        nc.vector.quantize_mx(
-            out=warm_codes[:].bitcast(FP8X4),
-            scales=warm_scales[:],
-            in_=bs_raw[:].rearrange("p g n -> p (g n)").bitcast(BF16),
-        )
-        for u in range(EARLY_WARM):
-            unread = psum.tile([P, WARM_COLS], F32, name="z", tag="z", bufs=4)
-            nc.tensor.matmul_mx(
-                out=unread[:],
-                lhsT=warm_codes[:, 0:P].bitcast(FP8X4),
-                lhsT_scale=warm_scales[:, 0:P],
-                rhs=warm_codes[:].bitcast(FP8X4),
-                rhs_scale=warm_scales[:],
-                start=True,
-                stop=True,
-            )
         nc.vector.memset(late[:].bitcast(I32), 0)
         def settle(h):
             for q in EARLY_QUADRANTS:
@@ -134,17 +115,6 @@ def tile_filter_bank_channel_mixer_s4_kernel(
         nc.sync.dma_start(out=bias_bf[:, :, 0:1], in_=bias.rearrange("(c p o) -> p c o", p=P, o=1))
         for i in range(2, len(WIDTHS)):
             load_x(nc.sync, i)
-        for u in range(WARM_PASSES):
-            unread = psum.tile([P, K_PASS], F32, name="z", tag="z", bufs=4)
-            nc.tensor.matmul_mx(
-                out=unread[:],
-                lhsT=b_raw[0][:, 0, 0 : 2 * P].bitcast(FP4X4),
-                lhsT_scale=bs_raw[:, 0, 0:P],
-                rhs=b_raw[0][:, 0, :].bitcast(FP4X4),
-                rhs_scale=bs_raw[:, 0, 0:K_PASS],
-                start=True,
-                stop=True,
-            )
 
 
         def deal(h, t0, t1):

@@ -22,7 +22,7 @@ K_PASS = P * PACK
 PASSES = 2
 WIDTHS = (512, 512, 512, 512)
 C_TILES = CHANNELS // P
-EARLY_QUADRANTS = (0, 2, 1, 3)
+WARM = 8
 MIX_DELAY = 6
 MIX_EVERY = 2
 VECTOR_EVERY = 3
@@ -58,9 +58,8 @@ def tile_filter_bank_channel_mixer_s4_kernel(
             bs_sb.append(dealt_scales)
         m_sb = keep.tile([P, PASSES, 4 * CHANNELS], U8, name="mixw", align_bytes=64)
         xs_head = keep.tile([P, PASSES, WIDTHS[0]], U8, name="xshead", align_bytes=64)
-        late = keep.tile([P, PASSES * (FRAMES - WIDTHS[0] + CHANNELS)], U8, name="late", align_bytes=64)
-        xs_rest = late[:, 0 : PASSES * (FRAMES - WIDTHS[0])].rearrange("p (g n) -> p g n", g=PASSES)
-        ms = late[:, PASSES * (FRAMES - WIDTHS[0]) :].rearrange("p (g n) -> p g n", g=PASSES)
+        xs_rest = keep.tile([P, PASSES, FRAMES - WIDTHS[0]], U8, name="xsrest", align_bytes=64)
+        ms = keep.tile([P, PASSES, CHANNELS], U8, name="ms", align_bytes=64)
         gain_bf = keep.tile([P, PASSES, PACK], BF16, name="gainbf")
         gain_f = keep.tile([P, PASSES, PACK], F32, name="gainf")
         sgn = keep.tile([P, PASSES, PACK], F32, name="sgn")
@@ -90,24 +89,31 @@ def tile_filter_bank_channel_mixer_s4_kernel(
                 in_=src[:, 4 * q : 4 * q + 4, first : first + count].rearrange("g r n -> r g n").bitcast(I32),
             )
 
-        bs_early = keep.tile([P, PASSES, FILTERS], U8, name="bsearly", align_bytes=64)
-        for q, eng in zip(EARLY_QUADRANTS, (nc.sync, nc.scalar, nc.sync, nc.scalar)):
-            load_quadrant(eng, bs_early, bank_scales, 0, FILTERS, q)
-        clear(nc.vector, xs_head)
+        xs_early = keep.tile([P, PASSES, WIDTHS[0]], U8, name="xsearly", align_bytes=64)
+        load_quadrant(nc.sync, xs_early, x_scales, 0, WIDTHS[0], 0)
+        load_quadrant(nc.scalar, xs_early, x_scales, 0, WIDTHS[0], 2)
         clear(nc.vector, bs_raw)
-        load_scales(nc.scalar, xs_head, x_scales, 0, WIDTHS[0], range(1))
+        clear(nc.vector, ms)
+        clear(nc.vector, xs_head)
+        clear(nc.vector, xs_rest)
+        for r in range(4):
+            load_scales(nc.scalar if r % 2 else nc.sync, bs_raw, bank_scales, 0, FILTERS, [r])
         load_words(nc.scalar, b_raw[0], bank_words, 0, 2 * K_PASS)
         load_x(nc.scalar, 0)
-        nc.scalar.dma_start(out=gain_bf[:], in_=gain.rearrange("(h p t) -> p h t", p=P, t=PACK))
-        load_scales(nc.sync, xs_head, x_scales, 0, WIDTHS[0], range(1, 4))
+        for q in (1, 3):
+            load_quadrant(nc.sync, xs_head, x_scales, 0, WIDTHS[0], q)
+        nc.sync.dma_start(out=gain_bf[:], in_=gain.rearrange("(h p t) -> p h t", p=P, t=PACK))
         load_words(nc.sync, b_raw[1], bank_words, 2 * K_PASS, 2 * K_PASS)
-        nc.vector.memset(late[:].bitcast(I32), 0)
-        def settle(h):
-            for q in EARLY_QUADRANTS:
-                rows, cols = slice(32 * q, 32 * q + 4), slice(K_PASS * h, K_PASS * (h + 1))
-                nc.vector.tensor_copy(out=bs_raw[rows, :, cols].bitcast(I32), in_=bs_early[rows, :, cols].bitcast(I32))
-
-        settle(0)
+        warm_z = psum.tile([P, 512], F32, name="z", tag="z", bufs=4)
+        cleared = ms[:].rearrange("p g n -> p (g n)")
+        for e in range(WARM):
+            nc.tensor.matmul_mx(
+                out=warm_z[:], lhsT=cleared[:, 0 : 2 * P].bitcast(FP4X4), lhsT_scale=cleared[:, 0:P],
+                rhs=cleared.bitcast(FP4X4), rhs_scale=cleared[:, 0:512], start=True, stop=True,
+            )
+        for q in (0, 2):
+            rows = slice(32 * q, 32 * q + 4)
+            nc.vector.tensor_copy(out=xs_head[rows].bitcast(I32), in_=xs_early[rows].bitcast(I32))
         load_scales(nc.sync, xs_rest, x_scales, WIDTHS[0], FRAMES - WIDTHS[0], range(4))
         load_x(nc.sync, 1)
         load_scales(nc.sync, ms, mix_scales, 0, CHANNELS, range(4))
@@ -116,12 +122,13 @@ def tile_filter_bank_channel_mixer_s4_kernel(
         for i in range(2, len(WIDTHS)):
             load_x(nc.sync, i)
 
-
-        def deal(h, t0, t1):
-            nc.vector.tensor_copy(
+        def deal_words(move, h, t0, t1):
+            move(
                 out=b_sb[h][:, t0:t1].bitcast(U16),
                 in_=b_raw[h][:].bitcast(U16).rearrange("p g (m t) -> p t g m", t=PACK)[:, t0:t1],
             )
+
+        def deal_scales(h, t0, t1):
             nc.vector.tensor_copy(
                 out=bs_sb[h][:, t0:t1],
                 in_=bs_raw[:].rearrange("p g (h m t) -> p h t g m", h=PASSES, t=PACK)[:, h, t0:t1],
@@ -207,12 +214,13 @@ def tile_filter_bank_channel_mixer_s4_kernel(
                 nc.scalar.activation(out=o[:], in_=z[:], func=ACT.Identity, bias=bias_bf[:, c, 0:1])
             nc.sync.dma_start(out=out[P * c : P * (c + 1), n0 : n0 + w], in_=o[:])
 
-        deal(0, 0, 1)
-        deal(0, 1, 2)
-        deal(0, 2, PACK)
-        settle(1)
-        deal(1, 0, 2)
-        deal(1, 2, PACK)
+        for t in range(PACK):
+            deal_words(nc.scalar.copy, 0, t, t + 1)
+        for h in range(PASSES):
+            deal_scales(h, 0, 2)
+            deal_scales(h, 2, PACK)
+        deal_words(nc.vector.tensor_copy, 1, 0, 2)
+        deal_words(nc.vector.tensor_copy, 1, 2, PACK)
         nc.scalar.activation(out=gain_f[:], in_=gain_bf[:], func=ACT.Abs)
         nc.scalar.activation(out=sgn[:], in_=gain_bf[:], func=ACT.Sign)
 

@@ -22,7 +22,7 @@ K_PASS = P * PACK
 PASSES = 2
 WIDTHS = (512, 512, 512, 512)
 C_TILES = CHANNELS // P
-WARM = 8
+WARM = 6
 MIX_DELAY = 6
 MIX_EVERY = 2
 VECTOR_EVERY = 3
@@ -92,14 +92,13 @@ def tile_filter_bank_channel_mixer_s4_kernel(
         xs_early = keep.tile([P, PASSES, WIDTHS[0]], U8, name="xsearly", align_bytes=64)
         load_quadrant(nc.sync, xs_early, x_scales, 0, WIDTHS[0], 0)
         load_quadrant(nc.scalar, xs_early, x_scales, 0, WIDTHS[0], 2)
-        clear(nc.vector, bs_raw)
+        load_words(nc.sync, b_raw[0], bank_words, 0, 2 * K_PASS)
         clear(nc.vector, ms)
+        clear(nc.vector, bs_raw)
         clear(nc.vector, xs_head)
         clear(nc.vector, xs_rest)
-        for r in range(4):
-            load_scales(nc.scalar if r % 2 else nc.sync, bs_raw, bank_scales, 0, FILTERS, [r])
-        load_words(nc.scalar, b_raw[0], bank_words, 0, 2 * K_PASS)
-        load_x(nc.scalar, 0)
+        load_scales(nc.sync, bs_raw, bank_scales, 0, FILTERS, range(4))
+        load_x(nc.sync, 0)
         for q in (1, 3):
             load_quadrant(nc.sync, xs_head, x_scales, 0, WIDTHS[0], q)
         nc.sync.dma_start(out=gain_bf[:], in_=gain.rearrange("(h p t) -> p h t", p=P, t=PACK))
@@ -216,11 +215,10 @@ def tile_filter_bank_channel_mixer_s4_kernel(
 
         for t in range(PACK):
             deal_words(nc.scalar.copy, 0, t, t + 1)
-        for h in range(PASSES):
-            deal_scales(h, 0, 2)
-            deal_scales(h, 2, PACK)
-        deal_words(nc.vector.tensor_copy, 1, 0, 2)
-        deal_words(nc.vector.tensor_copy, 1, 2, PACK)
+        for h, t0, t1 in ((0, 0, 1), (0, 1, 2), (0, 2, PACK), (1, 0, 2), (1, 2, PACK)):
+            deal_scales(h, t0, t1)
+        for t0 in (0, 2):
+            deal_words(nc.vector.tensor_copy, 1, t0, t0 + 2)
         nc.scalar.activation(out=gain_f[:], in_=gain_bf[:], func=ACT.Abs)
         nc.scalar.activation(out=sgn[:], in_=gain_bf[:], func=ACT.Sign)
 

@@ -93,11 +93,12 @@ def tile_filter_bank_channel_mixer_s4_kernel(
         load_quadrant(nc.sync, xs_early, x_scales, 0, WIDTHS[0], 0)
         load_quadrant(nc.scalar, xs_early, x_scales, 0, WIDTHS[0], 2)
         load_words(nc.sync, b_raw[0], bank_words, 0, 2 * K_PASS)
-        clear(nc.vector, ms)
         clear(nc.vector, bs_raw)
+        clear(nc.vector, ms)
         clear(nc.vector, xs_head)
         clear(nc.vector, xs_rest)
-        load_scales(nc.sync, bs_raw, bank_scales, 0, FILTERS, range(4))
+        for r in range(4):
+            load_scales(nc.scalar if r % 2 else nc.sync, bs_raw, bank_scales, 0, FILTERS, [r])
         load_x(nc.sync, 0)
         for q in (1, 3):
             load_quadrant(nc.sync, xs_head, x_scales, 0, WIDTHS[0], q)

@@ -20,22 +20,23 @@ P = 128
 PACK = 4
 K_PASS = P * PACK
 PASSES = 2
-WIDTHS = (512, 512, 512, 512)
+QUADRANT = 32
+CHUNK = 512
+CHUNKS = FRAMES // CHUNK
+HALF = CHUNK // 2
 C_TILES = CHANNELS // P
-WARM = 6
-MIX_DELAY = 6
+BANKS = 8
+WARM_UPS = 7
+FIRST_MIX_STEP = 17
 MIX_EVERY = 2
-VECTOR_EVERY = 3
-INTERLEAVE_AT = 0
-QUANTIZE_AT = 3
-EMPTY_AT = 3
+UNITS_ON_VECTOR = (2, 4, 6)
+STORE_PAIR = 2
 
 
 def tile_filter_bank_channel_mixer_s4_kernel(
     tc, x_words, x_scales, bank_words, bank_scales, gain, mix_words, mix_scales, bias, out
 ):
     nc = tc.nc
-    starts = [sum(WIDTHS[:i]) for i in range(len(WIDTHS))]
     with ExitStack() as ctx:
         keep = ctx.enter_context(tc.tile_pool(name="keep", bufs=1))
         work = ctx.enter_context(tc.tile_pool(name="work", bufs=3))
@@ -43,238 +44,243 @@ def tile_filter_bank_channel_mixer_s4_kernel(
         ctx.enter_context(nc.allow_non_contiguous_dma(reason="small gain and bias columns"))
         ctx.enter_context(tc.manual_schedule())
 
-        x_sb = []
-        for i, w in enumerate(WIDTHS):
-            xt = keep.tile([P, PASSES, 2 * w], U8, name="x%d" % i, align_bytes=64)
-            x_sb.append(xt)
-        bs_raw = keep.tile([P, PASSES, FILTERS], U8, name="bsraw", align_bytes=64)
-        b_raw, b_sb, bs_sb = [], [], []
+        x_codes = []
+        for i in range(CHUNKS):
+            chunk_codes = keep.tile([P, PASSES, 2 * CHUNK], U8, name="x%d" % i, align_bytes=64)
+            x_codes.append(chunk_codes)
+        bank_plane = keep.tile([P, PASSES, FILTERS], U8, name="bank_plane", align_bytes=64)
+        bank_codes, slot_codes, slot_planes = [], [], []
         for h in range(PASSES):
-            raw = keep.tile([P, PASSES, 2 * K_PASS], U8, name="braw%d" % h, align_bytes=64)
-            b_raw.append(raw)
-            dealt = keep.tile([P, PACK, PASSES, 2 * P], U8, name="b%d" % h, align_bytes=64)
-            b_sb.append(dealt)
-            dealt_scales = keep.tile([P, PACK, PASSES, P], U8, name="bs%d" % h, align_bytes=64)
-            bs_sb.append(dealt_scales)
-        m_sb = keep.tile([P, PASSES, 4 * CHANNELS], U8, name="mixw", align_bytes=64)
-        xs_head = keep.tile([P, PASSES, WIDTHS[0]], U8, name="xshead", align_bytes=64)
-        xs_rest = keep.tile([P, PASSES, FRAMES - WIDTHS[0]], U8, name="xsrest", align_bytes=64)
-        ms = keep.tile([P, PASSES, CHANNELS], U8, name="ms", align_bytes=64)
-        gain_bf = keep.tile([P, PASSES, PACK], BF16, name="gainbf")
-        gain_f = keep.tile([P, PASSES, PACK], F32, name="gainf")
-        sgn = keep.tile([P, PASSES, PACK], F32, name="sgn")
-        bias_bf = keep.tile([P, C_TILES, 2], BF16, name="biasbf")
+            as_loaded = keep.tile([P, PASSES, 2 * K_PASS], U8, name="bank_codes%d" % h, align_bytes=64)
+            bank_codes.append(as_loaded)
+            dealt_codes = keep.tile([P, PACK, PASSES, 2 * P], U8, name="slot_codes%d" % h, align_bytes=64)
+            slot_codes.append(dealt_codes)
+            dealt_plane = keep.tile([P, PACK, PASSES, P], U8, name="slot_planes%d" % h, align_bytes=64)
+            slot_planes.append(dealt_plane)
+        mix_codes = keep.tile([P, PASSES, 4 * CHANNELS], U8, name="mix_codes", align_bytes=64)
+        x_plane_first = keep.tile([P, PASSES, CHUNK], U8, name="x_plane_first", align_bytes=64)
+        x_plane_rest = keep.tile([P, PASSES, FRAMES - CHUNK], U8, name="x_plane_rest", align_bytes=64)
+        mix_plane = keep.tile([P, PASSES, CHANNELS], U8, name="mix_plane", align_bytes=64)
+        gain_bf = keep.tile([P, PASSES, PACK], BF16, name="gain_bf")
+        gain_abs = keep.tile([P, PASSES, PACK], F32, name="gain_abs")
+        gain_sign = keep.tile([P, PASSES, PACK], F32, name="gain_sign")
+        bias_bf = keep.tile([P, C_TILES, 2], BF16, name="bias_bf")
+        x_rows_early = keep.tile([P, PASSES, CHUNK], U8, name="x_rows_early", align_bytes=64)
 
-        def clear(eng, tile):
-            eng.memset(tile[:].rearrange("p g n -> p (g n)").bitcast(I32), 0)
+        def clear(plane):
+            nc.vector.memset(plane[:].rearrange("p g n -> p (g n)").bitcast(I32), 0)
 
-        def load_words(eng, tile, src, first, count):
-            eng.dma_start(
+        def load_codes(tile, src, first, count):
+            nc.sync.dma_start(
                 out=tile[:].bitcast(I32), in_=src[:, :, first : first + count].rearrange("g p b -> p g b").bitcast(I32)
             )
 
-        def load_scales(eng, tile, src, first, count, rows):
-            for r in rows:
-                eng.dma_start(
-                    out=tile[r:P:32].bitcast(I32),
-                    in_=src[:, :, first : first + count].rearrange("g (q r) n -> r q g n", r=4)[r].bitcast(I32),
-                )
-
-        def load_x(eng, i):
-            load_words(eng, x_sb[i], x_words, 2 * starts[i], 2 * WIDTHS[i])
-
-        def load_quadrant(eng, tile, src, first, count, q):
+        def load_scale_rows(eng, plane, src, first, count, r):
             eng.dma_start(
-                out=tile[32 * q : 32 * q + 4].bitcast(I32),
-                in_=src[:, 4 * q : 4 * q + 4, first : first + count].rearrange("g r n -> r g n").bitcast(I32),
+                out=plane[r:P:QUADRANT].bitcast(I32),
+                in_=src[:, :, first : first + count].rearrange("g (q r) n -> r q g n", r=4)[r].bitcast(I32),
             )
 
-        xs_early = keep.tile([P, PASSES, WIDTHS[0]], U8, name="xsearly", align_bytes=64)
-        load_quadrant(nc.sync, xs_early, x_scales, 0, WIDTHS[0], 0)
-        load_quadrant(nc.scalar, xs_early, x_scales, 0, WIDTHS[0], 2)
-        load_words(nc.sync, b_raw[0], bank_words, 0, 2 * K_PASS)
-        clear(nc.vector, bs_raw)
-        clear(nc.vector, ms)
-        clear(nc.vector, xs_head)
-        clear(nc.vector, xs_rest)
+        def load_scale_quadrant(eng, plane, src, count, q):
+            eng.dma_start(
+                out=plane[QUADRANT * q : QUADRANT * q + 4].bitcast(I32),
+                in_=src[:, 4 * q : 4 * q + 4, 0:count].rearrange("g r n -> r g n").bitcast(I32),
+            )
+
+        def load_frames(i):
+            load_codes(x_codes[i], x_words, 2 * CHUNK * i, 2 * CHUNK)
+
+        load_scale_quadrant(nc.sync, x_rows_early, x_scales, CHUNK, 0)
+        load_scale_quadrant(nc.scalar, x_rows_early, x_scales, CHUNK, 2)
+        load_codes(bank_codes[0], bank_words, 0, 2 * K_PASS)
+        for plane in (bank_plane, mix_plane, x_plane_first, x_plane_rest):
+            clear(plane)
         for r in range(4):
-            load_scales(nc.scalar if r % 2 else nc.sync, bs_raw, bank_scales, 0, FILTERS, [r])
-        load_x(nc.sync, 0)
+            load_scale_rows(nc.scalar if r % 2 else nc.sync, bank_plane, bank_scales, 0, FILTERS, r)
+        load_frames(0)
         for q in (1, 3):
-            load_quadrant(nc.sync, xs_head, x_scales, 0, WIDTHS[0], q)
+            load_scale_quadrant(nc.sync, x_plane_first, x_scales, CHUNK, q)
         nc.sync.dma_start(out=gain_bf[:], in_=gain.rearrange("(h p t) -> p h t", p=P, t=PACK))
-        load_words(nc.sync, b_raw[1], bank_words, 2 * K_PASS, 2 * K_PASS)
-        warm_z = psum.tile([P, 512], F32, name="z", tag="z", bufs=4)
-        cleared = ms[:].rearrange("p g n -> p (g n)")
-        for e in range(WARM):
-            nc.tensor.matmul_mx(
-                out=warm_z[:], lhsT=cleared[:, 0 : 2 * P].bitcast(FP4X4), lhsT_scale=cleared[:, 0:P],
-                rhs=cleared.bitcast(FP4X4), rhs_scale=cleared[:, 0:512], start=True, stop=True,
-            )
-        for q in (0, 2):
-            rows = slice(32 * q, 32 * q + 4)
-            nc.vector.tensor_copy(out=xs_head[rows].bitcast(I32), in_=xs_early[rows].bitcast(I32))
-        load_scales(nc.sync, xs_rest, x_scales, WIDTHS[0], FRAMES - WIDTHS[0], range(4))
-        load_x(nc.sync, 1)
-        load_scales(nc.sync, ms, mix_scales, 0, CHANNELS, range(4))
-        nc.sync.dma_start(out=m_sb[:], in_=mix_words.rearrange("g p n t -> p g (n t)"))
-        nc.sync.dma_start(out=bias_bf[:, :, 0:1], in_=bias.rearrange("(c p o) -> p c o", p=P, o=1))
-        for i in range(2, len(WIDTHS)):
-            load_x(nc.sync, i)
+        load_codes(bank_codes[1], bank_words, 2 * K_PASS, 2 * K_PASS)
 
-        def deal_words(move, h, t0, t1):
+        unread = psum.tile([P, CHUNK], F32, name="bank", tag="bank", bufs=BANKS)
+        zeros = mix_plane[:].rearrange("p g n -> p (g n)")
+        for e in range(WARM_UPS):
+            nc.tensor.matmul_mx(
+                out=unread[:],
+                lhsT=zeros[:, 0 : 2 * P].bitcast(FP4X4),
+                lhsT_scale=zeros[:, 0:P],
+                rhs=zeros.bitcast(FP4X4),
+                rhs_scale=zeros[:, 0:CHUNK],
+                start=True,
+                stop=True,
+            )
+
+        for q in (0, 2):
+            rows = slice(QUADRANT * q, QUADRANT * q + 4)
+            nc.vector.tensor_copy(out=x_plane_first[rows].bitcast(I32), in_=x_rows_early[rows].bitcast(I32))
+
+        for r in range(4):
+            load_scale_rows(nc.sync, x_plane_rest, x_scales, CHUNK, FRAMES - CHUNK, r)
+        load_frames(1)
+        for r in range(4):
+            load_scale_rows(nc.sync, mix_plane, mix_scales, 0, CHANNELS, r)
+        nc.sync.dma_start(out=mix_codes[:], in_=mix_words.rearrange("g p n t -> p g (n t)"))
+        nc.sync.dma_start(out=bias_bf[:, :, 0:1], in_=bias.rearrange("(c p o) -> p c o", p=P, o=1))
+        for i in range(2, CHUNKS):
+            load_frames(i)
+
+        def deal_codes(move, h, t0, t1):
             move(
-                out=b_sb[h][:, t0:t1].bitcast(U16),
-                in_=b_raw[h][:].bitcast(U16).rearrange("p g (m t) -> p t g m", t=PACK)[:, t0:t1],
+                out=slot_codes[h][:, t0:t1].bitcast(U16),
+                in_=bank_codes[h][:].bitcast(U16).rearrange("p g (m t) -> p t g m", t=PACK)[:, t0:t1],
             )
 
         def deal_scales(h, t0, t1):
             nc.vector.tensor_copy(
-                out=bs_sb[h][:, t0:t1],
-                in_=bs_raw[:].rearrange("p g (h m t) -> p h t g m", h=PASSES, t=PACK)[:, h, t0:t1],
+                out=slot_planes[h][:, t0:t1],
+                in_=bank_plane[:].rearrange("p g (h m t) -> p h t g m", h=PASSES, t=PACK)[:, h, t0:t1],
             )
 
-        sub, grouped, codes = {}, {}, {}
+        by_slot, interleaved, h_planes, results = {}, {}, {}, {}
 
-        def filter_unit(group, t):
+        def filter_step(group, t):
             i, h, first, w = group
-            n0 = starts[i] + first
-            y = psum.tile([P, w], F32, name="y", tag="y", bufs=4)
+            y = psum.tile([P, w], F32, name="bank", tag="bank", bufs=BANKS)
+            plane, n0 = (x_plane_first, first) if i == 0 else (x_plane_rest, CHUNK * (i - 1) + first)
             for g in range(PASSES):
                 nc.tensor.matmul_mx(
                     out=y[:],
-                    lhsT=b_sb[h][:, t, g, :].bitcast(FP4X4),
-                    lhsT_scale=bs_sb[h][:, t, g, :],
-                    rhs=x_sb[i][:, g, 2 * first : 2 * (first + w)].bitcast(FP4X4),
-                    rhs_scale=xs_head[:, g, n0 : n0 + w] if i == 0 else xs_rest[:, g, n0 - WIDTHS[0] : n0 - WIDTHS[0] + w],
+                    lhsT=slot_codes[h][:, t, g, :].bitcast(FP4X4),
+                    lhsT_scale=slot_planes[h][:, t, g, :],
+                    rhs=x_codes[i][:, g, 2 * first : 2 * (first + w)].bitcast(FP4X4),
+                    rhs_scale=plane[:, g, n0 : n0 + w],
                     start=(g == 0),
                     stop=(g == PASSES - 1),
                 )
             if t == 0:
-                s = work.tile([P, PACK, w], BF16, name="s", tag="s", bufs=10, align_bytes=64)
-                sub[group] = s
-            nc.scalar.activation(out=sub[group][:, t, :], in_=y[:], func=ACT.Abs, scale=gain_f[:, h, t : t + 1])
+                rectified = work.tile([P, PACK, w], BF16, name="s", tag="s", bufs=10, align_bytes=64)
+                by_slot[group] = rectified
+            nc.scalar.activation(out=by_slot[group][:, t, :], in_=y[:], func=ACT.Abs, scale=gain_abs[:, h, t : t + 1])
 
-        def sign(group, t):
-            rows = sub[group][:, t, :]
+        def apply_sign(group, t):
+            rows = by_slot[group][:, t, :]
             nc.vector.tensor_scalar(
-                out=rows, in0=rows, scalar1=sgn[:, group[1], t : t + 1], scalar2=None, op0=ALU.mult
+                out=rows, in0=rows, scalar1=gain_sign[:, group[1], t : t + 1], scalar2=None, op0=ALU.mult
             )
 
         def interleave(group, parts=1):
             w = group[3]
-            gr = work.tile([P, w, PACK], BF16, name="gr", tag="gr", bufs=10, align_bytes=64)
+            words = work.tile([P, w, PACK], BF16, name="gr", tag="gr", bufs=10, align_bytes=64)
             for e in range(parts):
                 cols = slice(e * w // parts, (e + 1) * w // parts)
                 nc.vector.tensor_copy(
-                    out=gr[:, cols, :].rearrange("p (c i) t -> p c t i", i=4),
-                    in_=sub[group][:, :, cols].rearrange("p t (c i) -> p c t i", i=4),
+                    out=words[:, cols, :].rearrange("p (c i) t -> p c t i", i=4),
+                    in_=by_slot[group][:, :, cols].rearrange("p t (c i) -> p c t i", i=4),
                 )
-            grouped[group] = gr
+            interleaved[group] = words
 
         def quantize(group, parts=1):
             i, h, first, w = group
             if first == 0:
-                c = work.tile([P, WIDTHS[i]], U32, name="hc", tag="hc", bufs=8, align_bytes=64)
-                sc = work.tile([P, WIDTHS[i]], U8, name="hs", tag="hs", bufs=8, align_bytes=64)
-                codes[(i, h)] = (c, sc)
-            c, sc = codes[(i, h)]
+                codes = work.tile([P, CHUNK], U32, name="hc", tag="hc", bufs=CHUNKS * PASSES, align_bytes=64)
+                plane = work.tile([P, CHUNK], U8, name="hs", tag="hs", bufs=CHUNKS * PASSES, align_bytes=64)
+                h_planes[(i, h)] = (codes, plane)
+            codes, plane = h_planes[(i, h)]
             for e in range(parts):
                 lo, hi = e * w // parts, (e + 1) * w // parts
                 nc.vector.quantize_mx(
-                    out=c[:, first + lo : first + hi].bitcast(FP8X4),
-                    scales=sc[:, first + lo : first + hi],
-                    in_=grouped[group][:, lo:hi, :].rearrange("p n t -> p (n t)"),
+                    out=codes[:, first + lo : first + hi].bitcast(FP8X4),
+                    scales=plane[:, first + lo : first + hi],
+                    in_=interleaved[group][:, lo:hi, :].rearrange("p n t -> p (n t)"),
                 )
 
-        def mix_pass(i, c, g, z, cols):
-            hc, hs = codes[(i, g)]
+        def mix_pass(i, c, h, z, cols):
+            codes, plane = h_planes[(i, h)]
             nc.tensor.matmul_mx(
                 out=z[:],
-                lhsT=m_sb[:, g, 4 * P * c : 4 * P * (c + 1)].bitcast(FP8X4),
-                lhsT_scale=ms[:, g, P * c : P * (c + 1)],
-                rhs=hc[:, cols].bitcast(FP8X4),
-                rhs_scale=hs[:, cols],
-                start=(g == 0),
-                stop=(g == PASSES - 1),
+                lhsT=mix_codes[:, h, 4 * P * c : 4 * P * (c + 1)].bitcast(FP8X4),
+                lhsT_scale=mix_plane[:, h, P * c : P * (c + 1)],
+                rhs=codes[:, cols].bitcast(FP8X4),
+                rhs_scale=plane[:, cols],
+                start=(h == 0),
+                stop=(h == PASSES - 1),
             )
 
-        def mix_unit(i, c, cols, tag="z"):
-            z = psum.tile([P, cols.stop - cols.start], F32, name=tag, tag=tag, bufs=4)
-            for g in range(PASSES):
-                mix_pass(i, c, g, z, cols)
+        def mix_unit(i, c):
+            z = psum.tile([P, CHUNK], F32, name="bank", tag="bank", bufs=BANKS)
+            for h in range(PASSES):
+                mix_pass(i, c, h, z, slice(0, CHUNK))
             return z
 
         def finish(i, c, cols, z, on_vector):
-            n0, w = starts[i] + cols.start, cols.stop - cols.start
-            o = work.tile([P, w], F32, name="o", tag="o", bufs=20, align_bytes=64)
+            n0, w = CHUNK * i + cols.start, cols.stop - cols.start
+            together = 1 if w == CHUNK else STORE_PAIR
+            c0 = c - c % together
+            if c == c0:
+                result = work.tile([P, together, w], F32, name="o", tag="o", bufs=CHUNKS * C_TILES, align_bytes=64)
+                results[(n0, c0)] = result
+            result = results[(n0, c0)]
             if on_vector:
-                nc.vector.tensor_scalar(out=o[:], in0=z[:], scalar1=bias_bf[:, c, 0:1], scalar2=None, op0=ALU.add)
+                nc.vector.tensor_scalar(
+                    out=result[:, c - c0, :], in0=z[:], scalar1=bias_bf[:, c, 0:1], scalar2=None, op0=ALU.add
+                )
             else:
-                nc.scalar.activation(out=o[:], in_=z[:], func=ACT.Identity, bias=bias_bf[:, c, 0:1])
-            nc.sync.dma_start(out=out[P * c : P * (c + 1), n0 : n0 + w], in_=o[:])
+                nc.scalar.activation(out=result[:, c - c0, :], in_=z[:], func=ACT.Identity, bias=bias_bf[:, c, 0:1])
+            if c == c0 + together - 1:
+                rows = out[P * c0 : P * (c0 + together), n0 : n0 + w]
+                nc.sync.dma_start(out=rows.rearrange("(c p) n -> p c n", p=P), in_=result[:])
 
         for t in range(PACK):
-            deal_words(nc.scalar.copy, 0, t, t + 1)
+            deal_codes(nc.scalar.copy, 0, t, t + 1)
         for h, t0, t1 in ((0, 0, 1), (0, 1, 2), (0, 2, PACK), (1, 0, 2), (1, 2, PACK)):
             deal_scales(h, t0, t1)
         for t0 in (0, 2):
-            deal_words(nc.vector.tensor_copy, 1, t0, t0 + 2)
-        nc.scalar.activation(out=gain_f[:], in_=gain_bf[:], func=ACT.Abs)
-        nc.scalar.activation(out=sgn[:], in_=gain_bf[:], func=ACT.Sign)
+            deal_codes(nc.vector.tensor_copy, 1, t0, t0 + 2)
+        nc.scalar.activation(out=gain_abs[:], in_=gain_bf[:], func=ACT.Abs)
+        nc.scalar.activation(out=gain_sign[:], in_=gain_bf[:], func=ACT.Sign)
 
-        groups = [(i, h, 0, w) for i, w in enumerate(WIDTHS) for h in range(PASSES)]
-        for at, cuts in ((len(groups) - 1, (256, 256)), (0, (512,))):
-            i, h, first, w = groups[at]
-            groups[at : at + 1] = [(i, h, sum(cuts[:e]), cuts[e]) for e in range(len(cuts))]
-        waiting = []
-        for_vector, held = [], []
-        step, last_mix, mixed = 0, -MIX_EVERY, 0
+        last = CHUNKS - 1
+        halves = [(last, PASSES - 1, first, HALF) for first in (0, HALF)]
+        groups = [(i, h, 0, CHUNK) for i in range(CHUNKS) for h in range(PASSES)][:-1] + halves
+        units = [(i, c) for i in range(last) for c in range(C_TILES)]
+        whole = slice(0, CHUNK)
+        for_vector = []
+        step, mixed = 0, 0
         for n, group in enumerate(groups):
             before = groups[n - 1] if n else None
             for t in range(PACK):
-                filter_unit(group, t)
-                if waiting and waiting[0][0] <= step and step - last_mix >= (MIX_EVERY if step < 32 else 1) and step < 99:
-                    first, mi, c, cols = waiting.pop(0)
-                    z = mix_unit(mi, c, cols)
-                    last_mix = step
+                filter_step(group, t)
+                if step >= FIRST_MIX_STEP and (step - FIRST_MIX_STEP) % MIX_EVERY == 0:
+                    i, c = units[mixed]
+                    z = mix_unit(i, c)
                     mixed += 1
-                    if n == len(groups) - 1 and t >= 4:
-                        held.append((mi, c, cols, z))
-                    elif mixed % VECTOR_EVERY == 0 and mixed <= 6:
-                        for_vector.append((mi, c, cols, z))
+                    if mixed in UNITS_ON_VECTOR:
+                        for_vector.append((i, c, whole, z))
                     else:
-                        finish(mi, c, cols, z, False)
-                if t == 0 and before and (INTERLEAVE_AT < 0 or n <= 1):
-                    interleave(before)
-                sign(group, t)
-                if t == EMPTY_AT and for_vector:
-                    finish(*for_vector.pop(0), True)
-                if t == INTERLEAVE_AT and before and n > 1:
-                    interleave(before)
-                if t == (QUANTIZE_AT if n < len(groups) - 1 else 3) and before:
-                    quantize(before)
-                    if before[1] == PASSES - 1:
-                        cols = slice(before[2], before[2] + before[3])
-                        waiting += [(step + MIX_DELAY + 0 * before[0], before[0], c, cols) for c in range(C_TILES)]
+                        finish(i, c, whole, z, False)
                 step += 1
-        last = groups[-1]
-        interleave(last, parts=2)
-        quantize(last, parts=2)
-        for item in for_vector + held:
-            finish(*item, False)
-        cols = slice(last[2], last[2] + last[3])
-        waiting += [(step, last[0], c, cols) for c in range(C_TILES)]
-        for first, mi, c, cols in [u for u in waiting if u[1] < last[0]]:
-            finish(mi, c, cols, mix_unit(mi, c, cols), False)
-        ending = [u for u in waiting if u[1] == last[0]]
-        for e in range(0, len(ending), C_TILES):
-            banks = []
-            for first, mi, c, cols in ending[e : e + C_TILES]:
-                tag = "y" if e == 0 else "z"
-                z = psum.tile([P, cols.stop - cols.start], F32, name=tag, tag=tag, bufs=4)
-                mix_pass(mi, c, 0, z, cols)
-                banks.append(z)
-            for (first, mi, c, cols), z in zip(ending[e : e + C_TILES], banks):
-                mix_pass(mi, c, 1, z, cols)
-                finish(mi, c, cols, z, e + C_TILES >= len(ending) and c % 2 == 0)
+                if t == 0 and n == 1:
+                    interleave(before)
+                apply_sign(group, t)
+                if t == PACK - 1 and for_vector:
+                    finish(*for_vector.pop(0), True)
+                if t == 0 and n > 1:
+                    interleave(before)
+                if t == PACK - 1 and before:
+                    quantize(before)
+        interleave(groups[-1], parts=2)
+        quantize(groups[-1], parts=2)
+        for i, c in units[mixed:]:
+            finish(i, c, whole, mix_unit(i, c), False)
+
+        for i, h, first, w in halves:
+            cols = slice(first, first + w)
+            sums = []
+            for c in range(C_TILES):
+                z = psum.tile([P, w], F32, name="bank", tag="bank", bufs=BANKS)
+                mix_pass(last, c, 0, z, cols)
+                sums.append(z)
+            for c in range(C_TILES):
+                mix_pass(last, c, 1, sums[c], cols)
+                finish(last, c, cols, sums[c], c % 2 == 1)

@@ -26,7 +26,8 @@ CHUNKS = FRAMES // CHUNK
 HALF = CHUNK // 2
 C_TILES = CHANNELS // P
 BANKS = 8
-WARM_UPS = 7
+SPAN = 256
+WARM_UPS = 6
 FIRST_MIX_STEP = 17
 MIX_EVERY = 2
 UNITS_ON_VECTOR = (2, 4, 6)
@@ -44,23 +45,32 @@ def tile_filter_bank_channel_mixer_s4_kernel(
         ctx.enter_context(nc.allow_non_contiguous_dma(reason="small gain and bias columns"))
         ctx.enter_context(tc.manual_schedule())
 
+        def placed(pool, shape, shift, name, bufs=1):
+            size = 1
+            for extent in shape[1:]:
+                size = size * extent
+            room = pool.tile([P, shift + size], U8, name=name, tag=name, bufs=bufs, align_bytes=SPAN)
+            names = " ".join("d%d" % e for e in range(len(shape) - 1))
+            sizes = {"d%d" % e: extent for e, extent in enumerate(shape[1:])}
+            return room[:, shift:].rearrange("p (%s) -> p %s" % (names, names), **sizes)
+
         x_codes = []
         for i in range(CHUNKS):
-            chunk_codes = keep.tile([P, PASSES, 2 * CHUNK], U8, name="x%d" % i, align_bytes=64)
+            chunk_codes = placed(keep, [P, PASSES, 2 * CHUNK], 0, "x%d" % i)
             x_codes.append(chunk_codes)
         bank_plane = keep.tile([P, PASSES, FILTERS], U8, name="bank_plane", align_bytes=64)
         bank_codes, slot_codes, slot_planes = [], [], []
         for h in range(PASSES):
             as_loaded = keep.tile([P, PASSES, 2 * K_PASS], U8, name="bank_codes%d" % h, align_bytes=64)
             bank_codes.append(as_loaded)
-            dealt_codes = keep.tile([P, PACK, PASSES, 2 * P], U8, name="slot_codes%d" % h, align_bytes=64)
+            dealt_codes = placed(keep, [P, PACK, PASSES, 2 * P], 192, "slot_codes%d" % h)
             slot_codes.append(dealt_codes)
-            dealt_plane = keep.tile([P, PACK, PASSES, P], U8, name="slot_planes%d" % h, align_bytes=64)
+            dealt_plane = placed(keep, [P, PACK, PASSES, 2 * P], 128, "slot_planes%d" % h)[:, :, :, 0:P]
             slot_planes.append(dealt_plane)
-        mix_codes = keep.tile([P, PASSES, 4 * CHANNELS], U8, name="mix_codes", align_bytes=64)
-        x_plane_first = keep.tile([P, PASSES, CHUNK], U8, name="x_plane_first", align_bytes=64)
-        x_plane_rest = keep.tile([P, PASSES, FRAMES - CHUNK], U8, name="x_plane_rest", align_bytes=64)
-        mix_plane = keep.tile([P, PASSES, CHANNELS], U8, name="mix_plane", align_bytes=64)
+        mix_codes = placed(keep, [P, PASSES, 4 * CHANNELS], 192, "mix_codes")
+        x_plane_first = placed(keep, [P, PASSES, CHUNK], 64, "x_plane_first")
+        x_plane_rest = placed(keep, [P, PASSES, FRAMES - CHUNK], 64, "x_plane_rest")
+        mix_plane = placed(keep, [P, PASSES, CHANNELS], 0, "mix_plane")
         gain_bf = keep.tile([P, PASSES, PACK], BF16, name="gain_bf")
         gain_abs = keep.tile([P, PASSES, PACK], F32, name="gain_abs")
         gain_sign = keep.tile([P, PASSES, PACK], F32, name="gain_sign")
@@ -183,8 +193,8 @@ def tile_filter_bank_channel_mixer_s4_kernel(
         def quantize(group, parts=1):
             i, h, first, w = group
             if first == 0:
-                codes = work.tile([P, CHUNK], U32, name="hc", tag="hc", bufs=CHUNKS * PASSES, align_bytes=64)
-                plane = work.tile([P, CHUNK], U8, name="hs", tag="hs", bufs=CHUNKS * PASSES, align_bytes=64)
+                codes = placed(work, [P, 4 * CHUNK], 64, "hc", CHUNKS * PASSES).bitcast(U32)
+                plane = placed(work, [P, CHUNK], 192, "hs", CHUNKS * PASSES)
                 h_planes[(i, h)] = (codes, plane)
             codes, plane = h_planes[(i, h)]
             for e in range(parts):

@@ -28,8 +28,9 @@ C_TILES = CHANNELS // P
 BANKS = 8
 SPAN = 256
 WARM_UPS = 6
-FIRST_MIX_STEP = 17
-MIX_EVERY = 2
+FIRST_MIX_STEP = 19
+MIX_EVERY = 4
+MIX_RUN = 2
 UNITS_ON_VECTOR = (2, 4, 6)
 STORE_PAIR = 2
 
@@ -262,13 +263,13 @@ def tile_filter_bank_channel_mixer_s4_kernel(
             for t in range(PACK):
                 filter_step(group, t)
                 if step >= FIRST_MIX_STEP and (step - FIRST_MIX_STEP) % MIX_EVERY == 0:
-                    i, c = units[mixed]
-                    z = mix_unit(i, c)
-                    mixed += 1
-                    if mixed in UNITS_ON_VECTOR:
-                        for_vector.append((i, c, whole, z))
-                    else:
-                        finish(i, c, whole, z, False)
+                    for i, c in units[mixed : mixed + MIX_RUN]:
+                        z = mix_unit(i, c)
+                        mixed += 1
+                        if mixed in UNITS_ON_VECTOR:
+                            for_vector.append((i, c, whole, z))
+                        else:
+                            finish(i, c, whole, z, False)
                 step += 1
                 if t == 0 and n == 1:
                     interleave(before)

@@ -73,8 +73,9 @@ def tile_filter_bank_channel_mixer_s4_kernel(
         x_plane_rest = placed(keep, [P, PASSES, FRAMES - CHUNK], 64, "x_plane_rest")
         mix_plane = placed(keep, [P, PASSES, CHANNELS], 0, "mix_plane")
         gain_bf = keep.tile([P, PASSES, PACK], BF16, name="gain_bf")
-        gain_abs = keep.tile([P, PASSES, PACK], F32, name="gain_abs")
-        gain_sign = keep.tile([P, PASSES, PACK], F32, name="gain_sign")
+        gain_f32 = keep.tile([P, PASSES, PACK], F32, name="gain_f32")
+        half_sign = keep.tile([P, PASSES, PACK], F32, name="half_sign")
+        first_abs = keep.tile([P, PACK, CHUNK], F32, name="first_abs", align_bytes=64)
         bias_bf = keep.tile([P, C_TILES, 2], BF16, name="bias_bf")
         x_rows_early = keep.tile([P, PASSES, CHUNK], U8, name="x_rows_early", align_bytes=64)
 
@@ -111,8 +112,8 @@ def tile_filter_bank_channel_mixer_s4_kernel(
         load_frames(0)
         for q in (1, 3):
             load_scale_quadrant(nc.sync, x_plane_first, x_scales, CHUNK, q)
-        nc.sync.dma_start(out=gain_bf[:], in_=gain.rearrange("(h p t) -> p h t", p=P, t=PACK))
         load_codes(bank_codes[1], bank_words, 2 * K_PASS, 2 * K_PASS)
+        nc.sync.dma_start(out=gain_bf[:], in_=gain.rearrange("(h p t) -> p h t", p=P, t=PACK))
 
         unread = psum.tile([P, CHUNK], F32, name="bank", tag="bank", bufs=BANKS)
         zeros = mix_plane[:].rearrange("p g n -> p (g n)")
@@ -172,13 +173,22 @@ def tile_filter_bank_channel_mixer_s4_kernel(
             if t == 0:
                 rectified = work.tile([P, PACK, w], BF16, name="s", tag="s", bufs=10, align_bytes=64)
                 by_slot[group] = rectified
-            nc.scalar.activation(out=by_slot[group][:, t, :], in_=y[:], func=ACT.Abs, scale=gain_abs[:, h, t : t + 1])
+            if (i, h) == (0, 0):
+                nc.scalar.activation(out=first_abs[:, t, :], in_=y[:], func=ACT.Abs)
+            else:
+                nc.scalar.activation(out=by_slot[group][:, t, :], in_=y[:], func=ACT.Abs, scale=gain_f32[:, h, t : t + 1])
 
         def apply_sign(group, t):
+            i, h, first, w = group
             rows = by_slot[group][:, t, :]
-            nc.vector.tensor_scalar(
-                out=rows, in0=rows, scalar1=gain_sign[:, group[1], t : t + 1], scalar2=None, op0=ALU.mult
-            )
+            if (i, h) == (0, 0):
+                nc.vector.tensor_scalar(
+                    out=rows, in0=first_abs[:, t, :], scalar1=gain_bf[:, h, t : t + 1], scalar2=None, op0=ALU.mult
+                )
+            else:
+                nc.vector.tensor_scalar(
+                    out=rows, in0=rows, scalar1=half_sign[:, h, t : t + 1], scalar2=2.0, op0=ALU.mult, op1=ALU.mult
+                )
 
         def interleave(group, parts=1):
             w = group[3]
@@ -248,8 +258,10 @@ def tile_filter_bank_channel_mixer_s4_kernel(
             deal_scales(h, t0, t1)
         for t0 in (0, 2):
             deal_codes(nc.vector.tensor_copy, 1, t0, t0 + 2)
-        nc.scalar.activation(out=gain_abs[:], in_=gain_bf[:], func=ACT.Abs)
-        nc.scalar.activation(out=gain_sign[:], in_=gain_bf[:], func=ACT.Sign)
+        nc.vector.tensor_copy(out=gain_f32[:], in_=gain_bf[:])
+        nc.vector.tensor_scalar(
+            out=half_sign[:], in0=gain_bf[:], scalar1=0.0, scalar2=0.5, op0=ALU.is_ge, op1=ALU.subtract
+        )
 
         last = CHUNKS - 1
         halves = [(last, PASSES - 1, first, HALF) for first in (0, HALF)]

@@ -59,9 +59,10 @@ def tile_filter_bank_channel_mixer_s4_kernel(
         for i in range(CHUNKS):
             chunk_codes = placed(keep, [P, PASSES, 2 * CHUNK], 0, "x%d" % i)
             x_codes.append(chunk_codes)
-        bank_plane = keep.tile([P, PASSES, FILTERS], U8, name="bank_plane", align_bytes=64)
-        bank_codes, slot_codes, slot_planes = [], [], []
+        bank_planes, bank_codes, slot_codes, slot_planes = [], [], [], []
         for h in range(PASSES):
+            scale_rows = keep.tile([P, PASSES, K_PASS], U8, name="bank_plane%d" % h, align_bytes=64)
+            bank_planes.append(scale_rows)
             as_loaded = keep.tile([P, PASSES, 2 * K_PASS], U8, name="bank_codes%d" % h, align_bytes=64)
             bank_codes.append(as_loaded)
             dealt_codes = placed(keep, [P, PACK, PASSES, 2 * P], 192, "slot_codes%d" % h)
@@ -74,7 +75,7 @@ def tile_filter_bank_channel_mixer_s4_kernel(
         mix_plane = placed(keep, [P, PASSES, CHANNELS], 0, "mix_plane")
         gain_bf = keep.tile([P, PASSES, PACK], BF16, name="gain_bf")
         gain_f32 = keep.tile([P, PASSES, PACK], F32, name="gain_f32")
-        half_sign = keep.tile([P, PASSES, PACK], F32, name="half_sign")
+        gain_sign = keep.tile([P, PASSES, PACK], F32, name="gain_sign")
         first_abs = keep.tile([P, PACK, CHUNK], F32, name="first_abs", align_bytes=64)
         bias_bf = keep.tile([P, C_TILES, 2], BF16, name="bias_bf")
         x_rows_early = keep.tile([P, PASSES, CHUNK], U8, name="x_rows_early", align_bytes=64)
@@ -105,13 +106,15 @@ def tile_filter_bank_channel_mixer_s4_kernel(
         load_scale_quadrant(nc.sync, x_rows_early, x_scales, CHUNK, 0)
         load_scale_quadrant(nc.scalar, x_rows_early, x_scales, CHUNK, 2)
         load_codes(bank_codes[0], bank_words, 0, 2 * K_PASS)
-        for plane in (bank_plane, mix_plane, x_plane_first, x_plane_rest):
+        for plane in (bank_planes[0], mix_plane, x_plane_first, bank_planes[1], x_plane_rest):
             clear(plane)
         for r in range(4):
-            load_scale_rows(nc.scalar if r % 2 else nc.sync, bank_plane, bank_scales, 0, FILTERS, r)
+            load_scale_rows(nc.scalar if r % 2 else nc.sync, bank_planes[0], bank_scales, 0, K_PASS, r)
         load_frames(0)
         for q in (1, 3):
             load_scale_quadrant(nc.sync, x_plane_first, x_scales, CHUNK, q)
+        for r in range(4):
+            load_scale_rows(nc.sync, bank_planes[1], bank_scales, K_PASS, K_PASS, r)
         load_codes(bank_codes[1], bank_words, 2 * K_PASS, 2 * K_PASS)
         nc.sync.dma_start(out=gain_bf[:], in_=gain.rearrange("(h p t) -> p h t", p=P, t=PACK))
 
@@ -151,7 +154,7 @@ def tile_filter_bank_channel_mixer_s4_kernel(
         def deal_scales(h, t0, t1):
             nc.vector.tensor_copy(
                 out=slot_planes[h][:, t0:t1],
-                in_=bank_plane[:].rearrange("p g (h m t) -> p h t g m", h=PASSES, t=PACK)[:, h, t0:t1],
+                in_=bank_planes[h][:].rearrange("p g (m t) -> p t g m", t=PACK)[:, t0:t1],
             )
 
         by_slot, interleaved, h_planes, results = {}, {}, {}, {}
@@ -178,6 +181,11 @@ def tile_filter_bank_channel_mixer_s4_kernel(
             else:
                 nc.scalar.activation(out=by_slot[group][:, t, :], in_=y[:], func=ACT.Abs, scale=gain_f32[:, h, t : t + 1])
 
+            if (i, h, first, t) == (0, 0, 0, 2):
+                nc.scalar.activation(out=gain_f32[:], in_=gain_bf[:], func=ACT.Copy)
+            if (i, h, first, t) == (0, 0, 0, 3):
+                nc.scalar.activation(out=gain_sign[:], in_=gain_bf[:], func=ACT.Sign)
+
         def apply_sign(group, t):
             i, h, first, w = group
             rows = by_slot[group][:, t, :]
@@ -187,7 +195,7 @@ def tile_filter_bank_channel_mixer_s4_kernel(
                 )
             else:
                 nc.vector.tensor_scalar(
-                    out=rows, in0=rows, scalar1=half_sign[:, h, t : t + 1], scalar2=2.0, op0=ALU.mult, op1=ALU.mult
+                    out=rows, in0=rows, scalar1=gain_sign[:, h, t : t + 1], scalar2=None, op0=ALU.mult
                 )
 
         def interleave(group, parts=1):
@@ -254,14 +262,13 @@ def tile_filter_bank_channel_mixer_s4_kernel(
 
         for t in range(PACK):
             deal_codes(nc.scalar.copy, 0, t, t + 1)
-        for h, t0, t1 in ((0, 0, 1), (0, 1, 2), (0, 2, PACK), (1, 0, 2), (1, 2, PACK)):
-            deal_scales(h, t0, t1)
-        for t0 in (0, 2):
-            deal_codes(nc.vector.tensor_copy, 1, t0, t0 + 2)
-        nc.vector.tensor_copy(out=gain_f32[:], in_=gain_bf[:])
-        nc.vector.tensor_scalar(
-            out=half_sign[:], in0=gain_bf[:], scalar1=0.0, scalar2=0.5, op0=ALU.is_ge, op1=ALU.subtract
-        )
+        for t0, t1 in ((0, 1), (1, 2), (2, PACK)):
+            deal_scales(0, t0, t1)
+        deal_scales(1, 0, 2)
+        for t in range(2):
+            deal_codes(nc.vector.tensor_copy, 1, t, t + 1)
+        deal_scales(1, 2, PACK)
+        deal_codes(nc.vector.tensor_copy, 1, 2, PACK)
 
         last = CHUNKS - 1
         halves = [(last, PASSES - 1, first, HALF) for first in (0, HALF)]

@@ -42,6 +42,7 @@ def tile_filter_bank_channel_mixer_s4_kernel(
     with ExitStack() as ctx:
         keep = ctx.enter_context(tc.tile_pool(name="keep", bufs=1))
         work = ctx.enter_context(tc.tile_pool(name="work", bufs=3))
+        once = ctx.enter_context(tc.tile_pool(name="once", bufs=1))
         psum = ctx.enter_context(tc.psum_pool(name="psum", bufs=4))
         ctx.enter_context(nc.allow_non_contiguous_dma(reason="small gain and bias columns"))
         ctx.enter_context(tc.manual_schedule())
@@ -59,10 +60,10 @@ def tile_filter_bank_channel_mixer_s4_kernel(
         for i in range(CHUNKS):
             chunk_codes = placed(keep, [P, PASSES, 2 * CHUNK], 0, "x%d" % i)
             x_codes.append(chunk_codes)
-        bank_planes, bank_codes, slot_codes, slot_planes = [], [], [], []
+        both_planes = keep.tile([P, PASSES, PASSES, K_PASS], U8, name="bank_plane", align_bytes=64)
+        bank_planes = [both_planes[:, h] for h in range(PASSES)]
+        bank_codes, slot_codes, slot_planes = [], [], []
         for h in range(PASSES):
-            scale_rows = keep.tile([P, PASSES, K_PASS], U8, name="bank_plane%d" % h, align_bytes=64)
-            bank_planes.append(scale_rows)
             as_loaded = keep.tile([P, PASSES, 2 * K_PASS], U8, name="bank_codes%d" % h, align_bytes=64)
             bank_codes.append(as_loaded)
             dealt_codes = placed(keep, [P, PACK, PASSES, 2 * P], 192, "slot_codes%d" % h)
@@ -76,7 +77,7 @@ def tile_filter_bank_channel_mixer_s4_kernel(
         gain_bf = keep.tile([P, PASSES, PACK], BF16, name="gain_bf")
         gain_f32 = keep.tile([P, PASSES, PACK], F32, name="gain_f32")
         gain_sign = keep.tile([P, PASSES, PACK], F32, name="gain_sign")
-        first_abs = keep.tile([P, PACK, CHUNK], F32, name="first_abs", align_bytes=64)
+        first_abs = once.tile([P, PACK, CHUNK], F32, name="first_abs", align_bytes=64)
         bias_bf = keep.tile([P, C_TILES, 2], BF16, name="bias_bf")
         x_rows_early = keep.tile([P, PASSES, CHUNK], U8, name="x_rows_early", align_bytes=64)
 

@@ -24,14 +24,16 @@ QUADRANT = 32
 CHUNK = 512
 CHUNKS = FRAMES // CHUNK
 HALF = CHUNK // 2
+PIECES = ((0, CHUNK), (CHUNK, HALF), (2 * CHUNK, CHUNK), (3 * CHUNK, CHUNK), (CHUNK + HALF, HALF))
 C_TILES = CHANNELS // P
+GROUPS = len(PIECES) * PASSES
+STORES = len(PIECES) * C_TILES
 BANKS = 8
 SPAN = 256
+PLANE_AT = 128
 WARM_UPS = 6
-FIRST_MIX_STEP = 19
-MIX_EVERY = 4
-MIX_RUN = 2
-UNITS_ON_VECTOR = (2, 4, 6)
+FIRST_MIX_GROUP = 4
+RUN_FRAMES = 2 * CHUNK
 STORE_PAIR = 2
 
 
@@ -60,26 +62,26 @@ def tile_filter_bank_channel_mixer_s4_kernel(
         for i in range(CHUNKS):
             chunk_codes = placed(keep, [P, PASSES, 2 * CHUNK], 0, "x%d" % i)
             x_codes.append(chunk_codes)
-        both_planes = keep.tile([P, PASSES, PASSES, K_PASS], U8, name="bank_plane", align_bytes=64)
+        both_planes = keep.tile([P, PASSES, PASSES, K_PASS], U8, name="bank_plane", align_bytes=SPAN)
         bank_planes = [both_planes[:, h] for h in range(PASSES)]
         bank_codes, slot_codes, slot_planes = [], [], []
         for h in range(PASSES):
-            as_loaded = keep.tile([P, PASSES, 2 * K_PASS], U8, name="bank_codes%d" % h, align_bytes=64)
+            as_loaded = keep.tile([P, PASSES, 2 * K_PASS], U8, name="bank_codes%d" % h, align_bytes=SPAN)
             bank_codes.append(as_loaded)
-            dealt_codes = placed(keep, [P, PACK, PASSES, 2 * P], 192, "slot_codes%d" % h)
+            dealt_codes = placed(keep, [P, PACK, PASSES, 2 * P], 0, "slot_codes%d" % h)
             slot_codes.append(dealt_codes)
-            dealt_plane = placed(keep, [P, PACK, PASSES, 2 * P], 128, "slot_planes%d" % h)[:, :, :, 0:P]
+            dealt_plane = placed(keep, [P, PACK, PASSES, 2 * P], PLANE_AT, "slot_planes%d" % h)[:, :, :, 0:P]
             slot_planes.append(dealt_plane)
-        mix_codes = placed(keep, [P, PASSES, 4 * CHANNELS], 192, "mix_codes")
-        x_plane_first = placed(keep, [P, PASSES, CHUNK], 64, "x_plane_first")
-        x_plane_rest = placed(keep, [P, PASSES, FRAMES - CHUNK], 64, "x_plane_rest")
-        mix_plane = placed(keep, [P, PASSES, CHANNELS], 0, "mix_plane")
+        mix_codes = placed(keep, [P, PASSES, 4 * CHANNELS], 0, "mix_codes")
+        x_plane_first = placed(keep, [P, PASSES, CHUNK], PLANE_AT, "x_plane_first")
+        x_plane_rest = placed(keep, [P, PASSES, FRAMES - CHUNK], PLANE_AT, "x_plane_rest")
+        mix_plane = placed(keep, [P, PASSES, CHANNELS], PLANE_AT, "mix_plane")
         gain_bf = keep.tile([P, PASSES, PACK], BF16, name="gain_bf")
         gain_f32 = keep.tile([P, PASSES, PACK], F32, name="gain_f32")
         gain_sign = keep.tile([P, PASSES, PACK], F32, name="gain_sign")
-        first_abs = once.tile([P, PACK, CHUNK], F32, name="first_abs", align_bytes=64)
+        first_abs = once.tile([P, PACK, CHUNK], F32, name="first_abs", align_bytes=SPAN)
         bias_bf = keep.tile([P, C_TILES, 2], BF16, name="bias_bf")
-        x_rows_early = keep.tile([P, PASSES, CHUNK], U8, name="x_rows_early", align_bytes=64)
+        x_rows_early = keep.tile([P, PASSES, CHUNK], U8, name="x_rows_early", align_bytes=SPAN)
 
         def clear(plane):
             nc.vector.memset(plane[:].rearrange("p g n -> p (g n)").bitcast(I32), 0)
@@ -161,36 +163,36 @@ def tile_filter_bank_channel_mixer_s4_kernel(
         by_slot, interleaved, h_planes, results = {}, {}, {}, {}
 
         def filter_step(group, t):
-            i, h, first, w = group
+            (n0, w), h = group
+            i, first = divmod(n0, CHUNK)
             y = psum.tile([P, w], F32, name="bank", tag="bank", bufs=BANKS)
-            plane, n0 = (x_plane_first, first) if i == 0 else (x_plane_rest, CHUNK * (i - 1) + first)
+            plane, m0 = (x_plane_first, n0) if i == 0 else (x_plane_rest, n0 - CHUNK)
             for g in range(PASSES):
                 nc.tensor.matmul_mx(
                     out=y[:],
                     lhsT=slot_codes[h][:, t, g, :].bitcast(FP4X4),
                     lhsT_scale=slot_planes[h][:, t, g, :],
                     rhs=x_codes[i][:, g, 2 * first : 2 * (first + w)].bitcast(FP4X4),
-                    rhs_scale=plane[:, g, n0 : n0 + w],
+                    rhs_scale=plane[:, g, m0 : m0 + w],
                     start=(g == 0),
                     stop=(g == PASSES - 1),
                 )
             if t == 0:
-                rectified = work.tile([P, PACK, w], BF16, name="s", tag="s", bufs=10, align_bytes=64)
+                rectified = work.tile([P, PACK, w], BF16, name="s", tag="s", bufs=GROUPS, align_bytes=SPAN)
                 by_slot[group] = rectified
-            if (i, h) == (0, 0):
+            if (n0, h) == (0, 0):
                 nc.scalar.activation(out=first_abs[:, t, :], in_=y[:], func=ACT.Abs)
             else:
                 nc.scalar.activation(out=by_slot[group][:, t, :], in_=y[:], func=ACT.Abs, scale=gain_f32[:, h, t : t + 1])
-
-            if (i, h, first, t) == (0, 0, 0, 2):
+            if (n0, h, t) == (0, 0, 2):
                 nc.scalar.activation(out=gain_f32[:], in_=gain_bf[:], func=ACT.Copy)
-            if (i, h, first, t) == (0, 0, 0, 3):
+            if (n0, h, t) == (0, 0, 3):
                 nc.scalar.activation(out=gain_sign[:], in_=gain_bf[:], func=ACT.Sign)
 
         def apply_sign(group, t):
-            i, h, first, w = group
+            (n0, w), h = group
             rows = by_slot[group][:, t, :]
-            if (i, h) == (0, 0):
+            if (n0, h) == (0, 0):
                 nc.vector.tensor_scalar(
                     out=rows, in0=first_abs[:, t, :], scalar1=gain_bf[:, h, t : t + 1], scalar2=None, op0=ALU.mult
                 )
@@ -200,8 +202,8 @@ def tile_filter_bank_channel_mixer_s4_kernel(
                 )
 
         def interleave(group, parts=1):
-            w = group[3]
-            words = work.tile([P, w, PACK], BF16, name="gr", tag="gr", bufs=10, align_bytes=64)
+            w = group[0][1]
+            words = work.tile([P, w, PACK], BF16, name="gr", tag="gr", bufs=GROUPS, align_bytes=SPAN)
             for e in range(parts):
                 cols = slice(e * w // parts, (e + 1) * w // parts)
                 nc.vector.tensor_copy(
@@ -211,53 +213,51 @@ def tile_filter_bank_channel_mixer_s4_kernel(
             interleaved[group] = words
 
         def quantize(group, parts=1):
-            i, h, first, w = group
-            if first == 0:
-                codes = placed(work, [P, 4 * CHUNK], 64, "hc", CHUNKS * PASSES).bitcast(U32)
-                plane = placed(work, [P, CHUNK], 192, "hs", CHUNKS * PASSES)
-                h_planes[(i, h)] = (codes, plane)
-            codes, plane = h_planes[(i, h)]
+            w = group[0][1]
+            codes = placed(work, [P, 4 * CHUNK], 0, "hc", GROUPS).bitcast(U32)
+            plane = placed(work, [P, CHUNK], PLANE_AT, "hs", GROUPS)
+            h_planes[group] = (codes, plane)
             for e in range(parts):
                 lo, hi = e * w // parts, (e + 1) * w // parts
                 nc.vector.quantize_mx(
-                    out=codes[:, first + lo : first + hi].bitcast(FP8X4),
-                    scales=plane[:, first + lo : first + hi],
+                    out=codes[:, lo:hi].bitcast(FP8X4),
+                    scales=plane[:, lo:hi],
                     in_=interleaved[group][:, lo:hi, :].rearrange("p n t -> p (n t)"),
                 )
 
-        def mix_pass(i, c, h, z, cols):
-            codes, plane = h_planes[(i, h)]
+        def mix_pass(piece, c, h, z):
+            codes, plane = h_planes[(piece, h)]
             nc.tensor.matmul_mx(
                 out=z[:],
                 lhsT=mix_codes[:, h, 4 * P * c : 4 * P * (c + 1)].bitcast(FP8X4),
                 lhsT_scale=mix_plane[:, h, P * c : P * (c + 1)],
-                rhs=codes[:, cols].bitcast(FP8X4),
-                rhs_scale=plane[:, cols],
+                rhs=codes[:, 0 : piece[1]].bitcast(FP8X4),
+                rhs_scale=plane[:, 0 : piece[1]],
                 start=(h == 0),
                 stop=(h == PASSES - 1),
             )
 
-        def mix_unit(i, c):
-            z = psum.tile([P, CHUNK], F32, name="bank", tag="bank", bufs=BANKS)
+        def mix_unit(piece, c):
+            z = psum.tile([P, piece[1]], F32, name="bank", tag="bank", bufs=BANKS)
             for h in range(PASSES):
-                mix_pass(i, c, h, z, slice(0, CHUNK))
+                mix_pass(piece, c, h, z)
             return z
 
-        def finish(i, c, cols, z, on_vector):
-            n0, w = CHUNK * i + cols.start, cols.stop - cols.start
-            together = 1 if w == CHUNK else STORE_PAIR
+        def finish(piece, c, z, on_vector, together):
+            n0, w = piece
             c0 = c - c % together
-            if c == c0:
-                result = work.tile([P, together, w], F32, name="o", tag="o", bufs=CHUNKS * C_TILES, align_bytes=64)
-                results[(n0, c0)] = result
-            result = results[(n0, c0)]
+            if (n0, c0) not in results:
+                result = work.tile([P, together, w], F32, name="o", tag="o", bufs=STORES, align_bytes=SPAN)
+                results[(n0, c0)] = [result, 0]
+            result = results[(n0, c0)][0]
             if on_vector:
                 nc.vector.tensor_scalar(
                     out=result[:, c - c0, :], in0=z[:], scalar1=bias_bf[:, c, 0:1], scalar2=None, op0=ALU.add
                 )
             else:
                 nc.scalar.activation(out=result[:, c - c0, :], in_=z[:], func=ACT.Identity, bias=bias_bf[:, c, 0:1])
-            if c == c0 + together - 1:
+            results[(n0, c0)][1] += 1
+            if results[(n0, c0)][1] == together:
                 rows = out[P * c0 : P * (c0 + together), n0 : n0 + w]
                 nc.sync.dma_start(out=rows.rearrange("(c p) n -> p c n", p=P), in_=result[:])
 
@@ -271,47 +271,38 @@ def tile_filter_bank_channel_mixer_s4_kernel(
         deal_scales(1, 2, PACK)
         deal_codes(nc.vector.tensor_copy, 1, 2, PACK)
 
-        last = CHUNKS - 1
-        halves = [(last, PASSES - 1, first, HALF) for first in (0, HALF)]
-        groups = [(i, h, 0, CHUNK) for i in range(CHUNKS) for h in range(PASSES)][:-1] + halves
-        units = [(i, c) for i in range(last) for c in range(C_TILES)]
-        whole = slice(0, CHUNK)
-        for_vector = []
-        step, mixed = 0, 0
+        groups = [(piece, h) for piece in PIECES for h in range(PASSES)]
+        units = [(piece, c) for piece in PIECES[:-1] for c in range(C_TILES)]
         for n, group in enumerate(groups):
             before = groups[n - 1] if n else None
+            wide = group[0][1] == CHUNK
+            quantize_slot = 1 if wide and before in interleaved else PACK - 1
             for t in range(PACK):
                 filter_step(group, t)
-                if step >= FIRST_MIX_STEP and (step - FIRST_MIX_STEP) % MIX_EVERY == 0:
-                    for i, c in units[mixed : mixed + MIX_RUN]:
-                        z = mix_unit(i, c)
-                        mixed += 1
-                        if mixed in UNITS_ON_VECTOR:
-                            for_vector.append((i, c, whole, z))
-                        else:
-                            finish(i, c, whole, z, False)
-                step += 1
                 if t == 0 and n == 1:
                     interleave(before)
                 apply_sign(group, t)
-                if t == PACK - 1 and for_vector:
-                    finish(*for_vector.pop(0), True)
-                if t == 0 and n > 1:
+                if t == 0 and before and before not in interleaved:
                     interleave(before)
-                if t == PACK - 1 and before:
+                if t == quantize_slot and before:
                     quantize(before)
+            if wide and n >= FIRST_MIX_GROUP:
+                run = RUN_FRAMES // units[0][0][1]
+                for e in range(run):
+                    piece, c = units.pop(0)
+                    together = 1 if piece[1] == CHUNK else STORE_PAIR
+                    finish(piece, c, mix_unit(piece, c), e == run - 1, together)
+                interleave(group)
         interleave(groups[-1], parts=2)
         quantize(groups[-1], parts=2)
-        for i, c in units[mixed:]:
-            finish(i, c, whole, mix_unit(i, c), False)
+        for piece, c in units:
+            finish(piece, c, mix_unit(piece, c), False, 1)
 
-        for i, h, first, w in halves:
-            cols = slice(first, first + w)
-            sums = []
-            for c in range(C_TILES):
-                z = psum.tile([P, w], F32, name="bank", tag="bank", bufs=BANKS)
-                mix_pass(last, c, 0, z, cols)
-                sums.append(z)
-            for c in range(C_TILES):
-                mix_pass(last, c, 1, sums[c], cols)
-                finish(last, c, cols, sums[c], c % 2 == 1)
+        sums = []
+        for c in range(C_TILES):
+            z = psum.tile([P, HALF], F32, name="bank", tag="bank", bufs=BANKS)
+            mix_pass(PIECES[-1], c, 0, z)
+            sums.append(z)
+        for c in range(C_TILES):
+            mix_pass(PIECES[-1], c, 1, sums[c])
+            finish(PIECES[-1], c, sums[c], c % 2 == 0, 1)

@@ -23,18 +23,15 @@ PASSES = 2
 QUADRANT = 32
 CHUNK = 512
 CHUNKS = FRAMES // CHUNK
-HALF = CHUNK // 2
-PIECES = ((0, CHUNK), (CHUNK, HALF), (2 * CHUNK, CHUNK), (3 * CHUNK, CHUNK), (CHUNK + HALF, HALF))
 C_TILES = CHANNELS // P
-GROUPS = len(PIECES) * PASSES
-STORES = len(PIECES) * C_TILES
+GROUPS = CHUNKS * PASSES
 BANKS = 8
 SPAN = 256
 PLANE_AT = 128
 WARM_UPS = 6
-FIRST_MIX_GROUP = 4
-RUN_FRAMES = 2 * CHUNK
-STORE_PAIR = 2
+MIX_GROUPS = (4, 5)
+MIX_RUN = 2
+AHEAD = 2
 
 
 def tile_filter_bank_channel_mixer_s4_kernel(
@@ -160,39 +157,38 @@ def tile_filter_bank_channel_mixer_s4_kernel(
                 in_=bank_planes[h][:].rearrange("p g (m t) -> p t g m", t=PACK)[:, t0:t1],
             )
 
-        by_slot, interleaved, h_planes, results = {}, {}, {}, {}
+        by_slot, interleaved, h_planes = {}, {}, {}
 
         def filter_step(group, t):
-            (n0, w), h = group
-            i, first = divmod(n0, CHUNK)
-            y = psum.tile([P, w], F32, name="bank", tag="bank", bufs=BANKS)
-            plane, m0 = (x_plane_first, n0) if i == 0 else (x_plane_rest, n0 - CHUNK)
+            i, h = group
+            y = psum.tile([P, CHUNK], F32, name="bank", tag="bank", bufs=BANKS)
+            plane, n0 = (x_plane_first, 0) if i == 0 else (x_plane_rest, CHUNK * (i - 1))
             for g in range(PASSES):
                 nc.tensor.matmul_mx(
                     out=y[:],
                     lhsT=slot_codes[h][:, t, g, :].bitcast(FP4X4),
                     lhsT_scale=slot_planes[h][:, t, g, :],
-                    rhs=x_codes[i][:, g, 2 * first : 2 * (first + w)].bitcast(FP4X4),
-                    rhs_scale=plane[:, g, m0 : m0 + w],
+                    rhs=x_codes[i][:, g, :].bitcast(FP4X4),
+                    rhs_scale=plane[:, g, n0 : n0 + CHUNK],
                     start=(g == 0),
                     stop=(g == PASSES - 1),
                 )
             if t == 0:
-                rectified = work.tile([P, PACK, w], BF16, name="s", tag="s", bufs=GROUPS, align_bytes=SPAN)
+                rectified = work.tile([P, PACK, CHUNK], BF16, name="s", tag="s", bufs=GROUPS, align_bytes=SPAN)
                 by_slot[group] = rectified
-            if (n0, h) == (0, 0):
+            if group == (0, 0):
                 nc.scalar.activation(out=first_abs[:, t, :], in_=y[:], func=ACT.Abs)
             else:
                 nc.scalar.activation(out=by_slot[group][:, t, :], in_=y[:], func=ACT.Abs, scale=gain_f32[:, h, t : t + 1])
-            if (n0, h, t) == (0, 0, 2):
+            if (i, h, t) == (0, 0, 2):
                 nc.scalar.activation(out=gain_f32[:], in_=gain_bf[:], func=ACT.Copy)
-            if (n0, h, t) == (0, 0, 3):
+            if (i, h, t) == (0, 0, 3):
                 nc.scalar.activation(out=gain_sign[:], in_=gain_bf[:], func=ACT.Sign)
 
         def apply_sign(group, t):
-            (n0, w), h = group
+            h = group[1]
             rows = by_slot[group][:, t, :]
-            if (n0, h) == (0, 0):
+            if group == (0, 0):
                 nc.vector.tensor_scalar(
                     out=rows, in0=first_abs[:, t, :], scalar1=gain_bf[:, h, t : t + 1], scalar2=None, op0=ALU.mult
                 )
@@ -202,10 +198,9 @@ def tile_filter_bank_channel_mixer_s4_kernel(
                 )
 
         def interleave(group, parts=1):
-            w = group[0][1]
-            words = work.tile([P, w, PACK], BF16, name="gr", tag="gr", bufs=GROUPS, align_bytes=SPAN)
+            words = work.tile([P, CHUNK, PACK], BF16, name="gr", tag="gr", bufs=GROUPS, align_bytes=SPAN)
             for e in range(parts):
-                cols = slice(e * w // parts, (e + 1) * w // parts)
+                cols = slice(e * CHUNK // parts, (e + 1) * CHUNK // parts)
                 nc.vector.tensor_copy(
                     out=words[:, cols, :].rearrange("p (c i) t -> p c t i", i=4),
                     in_=by_slot[group][:, :, cols].rearrange("p t (c i) -> p c t i", i=4),
@@ -213,53 +208,42 @@ def tile_filter_bank_channel_mixer_s4_kernel(
             interleaved[group] = words
 
         def quantize(group, parts=1):
-            w = group[0][1]
             codes = placed(work, [P, 4 * CHUNK], 0, "hc", GROUPS).bitcast(U32)
             plane = placed(work, [P, CHUNK], PLANE_AT, "hs", GROUPS)
             h_planes[group] = (codes, plane)
             for e in range(parts):
-                lo, hi = e * w // parts, (e + 1) * w // parts
+                cols = slice(e * CHUNK // parts, (e + 1) * CHUNK // parts)
                 nc.vector.quantize_mx(
-                    out=codes[:, lo:hi].bitcast(FP8X4),
-                    scales=plane[:, lo:hi],
-                    in_=interleaved[group][:, lo:hi, :].rearrange("p n t -> p (n t)"),
+                    out=codes[:, cols].bitcast(FP8X4),
+                    scales=plane[:, cols],
+                    in_=interleaved[group][:, cols, :].rearrange("p n t -> p (n t)"),
                 )
 
-        def mix_pass(piece, c, h, z):
-            codes, plane = h_planes[(piece, h)]
+        def mix_pass(i, c, h, z):
+            codes, plane = h_planes[(i, h)]
             nc.tensor.matmul_mx(
                 out=z[:],
                 lhsT=mix_codes[:, h, 4 * P * c : 4 * P * (c + 1)].bitcast(FP8X4),
                 lhsT_scale=mix_plane[:, h, P * c : P * (c + 1)],
-                rhs=codes[:, 0 : piece[1]].bitcast(FP8X4),
-                rhs_scale=plane[:, 0 : piece[1]],
+                rhs=codes.bitcast(FP8X4),
+                rhs_scale=plane,
                 start=(h == 0),
                 stop=(h == PASSES - 1),
             )
 
-        def mix_unit(piece, c):
-            z = psum.tile([P, piece[1]], F32, name="bank", tag="bank", bufs=BANKS)
-            for h in range(PASSES):
-                mix_pass(piece, c, h, z)
+        def first_mix_pass(i, c):
+            z = psum.tile([P, CHUNK], F32, name="bank", tag="bank", bufs=BANKS)
+            mix_pass(i, c, 0, z)
             return z
 
-        def finish(piece, c, z, on_vector, together):
-            n0, w = piece
-            c0 = c - c % together
-            if (n0, c0) not in results:
-                result = work.tile([P, together, w], F32, name="o", tag="o", bufs=STORES, align_bytes=SPAN)
-                results[(n0, c0)] = [result, 0]
-            result = results[(n0, c0)][0]
+        def finish(i, c, z, on_vector):
+            mix_pass(i, c, 1, z)
+            result = work.tile([P, CHUNK], F32, name="o", tag="o", bufs=CHUNKS * C_TILES, align_bytes=SPAN)
             if on_vector:
-                nc.vector.tensor_scalar(
-                    out=result[:, c - c0, :], in0=z[:], scalar1=bias_bf[:, c, 0:1], scalar2=None, op0=ALU.add
-                )
+                nc.vector.tensor_scalar(out=result[:], in0=z[:], scalar1=bias_bf[:, c, 0:1], scalar2=None, op0=ALU.add)
             else:
-                nc.scalar.activation(out=result[:, c - c0, :], in_=z[:], func=ACT.Identity, bias=bias_bf[:, c, 0:1])
-            results[(n0, c0)][1] += 1
-            if results[(n0, c0)][1] == together:
-                rows = out[P * c0 : P * (c0 + together), n0 : n0 + w]
-                nc.sync.dma_start(out=rows.rearrange("(c p) n -> p c n", p=P), in_=result[:])
+                nc.scalar.activation(out=result[:], in_=z[:], func=ACT.Identity, bias=bias_bf[:, c, 0:1])
+            nc.sync.dma_start(out=out[P * c : P * (c + 1), CHUNK * i : CHUNK * (i + 1)], in_=result[:])
 
         for t in range(PACK):
             deal_codes(nc.scalar.copy, 0, t, t + 1)
@@ -271,12 +255,11 @@ def tile_filter_bank_channel_mixer_s4_kernel(
         deal_scales(1, 2, PACK)
         deal_codes(nc.vector.tensor_copy, 1, 2, PACK)
 
-        groups = [(piece, h) for piece in PIECES for h in range(PASSES)]
-        units = [(piece, c) for piece in PIECES[:-1] for c in range(C_TILES)]
+        last = CHUNKS - 1
+        groups = [(i, h) for i in range(CHUNKS) for h in range(PASSES)]
+        units = [(i, c) for i in range(last) for c in range(C_TILES)]
         for n, group in enumerate(groups):
             before = groups[n - 1] if n else None
-            wide = group[0][1] == CHUNK
-            quantize_slot = 1 if wide and before in interleaved else PACK - 1
             for t in range(PACK):
                 filter_step(group, t)
                 if t == 0 and n == 1:
@@ -284,25 +267,18 @@ def tile_filter_bank_channel_mixer_s4_kernel(
                 apply_sign(group, t)
                 if t == 0 and before and before not in interleaved:
                     interleave(before)
-                if t == quantize_slot and before:
-                    quantize(before)
-            if wide and n >= FIRST_MIX_GROUP:
-                run = RUN_FRAMES // units[0][0][1]
-                for e in range(run):
-                    piece, c = units.pop(0)
-                    together = 1 if piece[1] == CHUNK else STORE_PAIR
-                    finish(piece, c, mix_unit(piece, c), e == run - 1, together)
+            if before:
+                quantize(before)
+            if n in MIX_GROUPS:
+                for e in range(MIX_RUN):
+                    i, c = units.pop(0)
+                    finish(i, c, first_mix_pass(i, c), e == MIX_RUN - 1)
                 interleave(group)
         interleave(groups[-1], parts=2)
         quantize(groups[-1], parts=2)
-        for piece, c in units:
-            finish(piece, c, mix_unit(piece, c), False, 1)
+        for i, c in units:
+            finish(i, c, first_mix_pass(i, c), False)
 
-        sums = []
+        ahead = [first_mix_pass(last, c) for c in range(AHEAD)]
         for c in range(C_TILES):
-            z = psum.tile([P, HALF], F32, name="bank", tag="bank", bufs=BANKS)
-            mix_pass(PIECES[-1], c, 0, z)
-            sums.append(z)
-        for c in range(C_TILES):
-            mix_pass(PIECES[-1], c, 1, sums[c])
-            finish(PIECES[-1], c, sums[c], c % 2 == 0, 1)
+            finish(last, c, ahead[c] if c < AHEAD else first_mix_pass(last, c), c % 2 == 0)

@@ -18,6 +18,7 @@ ACT = mybir.ActivationFunctionType
 
 P = 128
 PACK = 4
+LAST_SLOT = PACK - 1
 K_PASS = P * PACK
 PASSES = 2
 QUADRANT = 32
@@ -29,7 +30,7 @@ BANKS = 8
 SPAN = 256
 PLANE_AT = 128
 WARM_UPS = 6
-MIX_GROUPS = (4, 5)
+MIX_GROUPS = (4, 5, 6)
 MIX_RUN = 2
 AHEAD = 2
 
@@ -75,8 +76,10 @@ def tile_filter_bank_channel_mixer_s4_kernel(
         mix_plane = placed(keep, [P, PASSES, CHANNELS], PLANE_AT, "mix_plane")
         gain_bf = keep.tile([P, PASSES, PACK], BF16, name="gain_bf")
         gain_f32 = keep.tile([P, PASSES, PACK], F32, name="gain_f32")
-        gain_sign = keep.tile([P, PASSES, PACK], F32, name="gain_sign")
-        first_abs = once.tile([P, PACK, CHUNK], F32, name="first_abs", align_bytes=SPAN)
+        below_zero = keep.tile([P, PASSES, PACK], BF16, name="below_zero")
+        gain_sign = keep.tile([P, PASSES, PACK], BF16, name="gain_sign")
+        sign_ratio = keep.tile([P, PASSES, PACK], BF16, name="sign_ratio")
+        first_abs = once.tile([P, LAST_SLOT, CHUNK], F32, name="first_abs", align_bytes=SPAN)
         bias_bf = keep.tile([P, C_TILES, 2], BF16, name="bias_bf")
         x_rows_early = keep.tile([P, PASSES, CHUNK], U8, name="x_rows_early", align_bytes=SPAN)
 
@@ -176,34 +179,38 @@ def tile_filter_bank_channel_mixer_s4_kernel(
             if t == 0:
                 rectified = work.tile([P, PACK, CHUNK], BF16, name="s", tag="s", bufs=GROUPS, align_bytes=SPAN)
                 by_slot[group] = rectified
-            if group == (0, 0):
+            if group == (0, 0) and t < LAST_SLOT:
                 nc.scalar.activation(out=first_abs[:, t, :], in_=y[:], func=ACT.Abs)
             else:
                 nc.scalar.activation(out=by_slot[group][:, t, :], in_=y[:], func=ACT.Abs, scale=gain_f32[:, h, t : t + 1])
-            if (i, h, t) == (0, 0, 2):
-                nc.scalar.activation(out=gain_f32[:], in_=gain_bf[:], func=ACT.Copy)
-            if (i, h, t) == (0, 0, 3):
-                nc.scalar.activation(out=gain_sign[:], in_=gain_bf[:], func=ACT.Sign)
 
         def apply_sign(group, t):
             h = group[1]
             rows = by_slot[group][:, t, :]
             if group == (0, 0):
                 nc.vector.tensor_scalar(
-                    out=rows, in0=first_abs[:, t, :], scalar1=gain_bf[:, h, t : t + 1], scalar2=None, op0=ALU.mult
+                    out=rows,
+                    in0=first_abs[:, t, :],
+                    scalar1=gain_bf[:, h, t : t + 1],
+                    scalar2=gain_sign[:, h, LAST_SLOT:],
+                    op0=ALU.mult,
+                    op1=ALU.mult,
                 )
             else:
                 nc.vector.tensor_scalar(
-                    out=rows, in0=rows, scalar1=gain_sign[:, h, t : t + 1], scalar2=None, op0=ALU.mult
+                    out=rows, in0=rows, scalar1=sign_ratio[:, h, t : t + 1], scalar2=None, op0=ALU.mult
                 )
 
         def interleave(group, parts=1):
             words = work.tile([P, CHUNK, PACK], BF16, name="gr", tag="gr", bufs=GROUPS, align_bytes=SPAN)
             for e in range(parts):
                 cols = slice(e * CHUNK // parts, (e + 1) * CHUNK // parts)
-                nc.vector.tensor_copy(
+                nc.vector.tensor_scalar(
                     out=words[:, cols, :].rearrange("p (c i) t -> p c t i", i=4),
-                    in_=by_slot[group][:, :, cols].rearrange("p t (c i) -> p c t i", i=4),
+                    in0=by_slot[group][:, :, cols].rearrange("p t (c i) -> p c t i", i=4),
+                    scalar1=gain_sign[:, group[1], LAST_SLOT:],
+                    scalar2=None,
+                    op0=ALU.mult,
                 )
             interleaved[group] = words
 
@@ -236,14 +243,17 @@ def tile_filter_bank_channel_mixer_s4_kernel(
             mix_pass(i, c, 0, z)
             return z
 
-        def finish(i, c, z, on_vector):
-            mix_pass(i, c, 1, z)
+        def empty(i, c, z, on_vector):
             result = work.tile([P, CHUNK], F32, name="o", tag="o", bufs=CHUNKS * C_TILES, align_bytes=SPAN)
             if on_vector:
                 nc.vector.tensor_scalar(out=result[:], in0=z[:], scalar1=bias_bf[:, c, 0:1], scalar2=None, op0=ALU.add)
             else:
                 nc.scalar.activation(out=result[:], in_=z[:], func=ACT.Identity, bias=bias_bf[:, c, 0:1])
             nc.sync.dma_start(out=out[P * c : P * (c + 1), CHUNK * i : CHUNK * (i + 1)], in_=result[:])
+
+        def finish(i, c, z, on_vector):
+            mix_pass(i, c, 1, z)
+            empty(i, c, z, on_vector)
 
         for t in range(PACK):
             deal_codes(nc.scalar.copy, 0, t, t + 1)
@@ -253,27 +263,43 @@ def tile_filter_bank_channel_mixer_s4_kernel(
         for t in range(2):
             deal_codes(nc.vector.tensor_copy, 1, t, t + 1)
         deal_scales(1, 2, PACK)
+        nc.vector.tensor_scalar(out=below_zero[:], in0=gain_bf[:], scalar1=0.0, scalar2=-2.0, op0=ALU.is_lt, op1=ALU.mult)
+        nc.vector.tensor_copy(out=gain_f32[:], in_=gain_bf[:])
         deal_codes(nc.vector.tensor_copy, 1, 2, PACK)
+        nc.vector.tensor_scalar(out=gain_sign[:], in0=below_zero[:], scalar1=1.0, scalar2=None, op0=ALU.add)
 
         last = CHUNKS - 1
         groups = [(i, h) for i in range(CHUNKS) for h in range(PASSES)]
         units = [(i, c) for i in range(last) for c in range(C_TILES)]
+        for_vector = []
         for n, group in enumerate(groups):
             before = groups[n - 1] if n else None
+            if before:
+                interleave(before)
+            if for_vector:
+                empty(*for_vector.pop(), True)
             for t in range(PACK):
                 filter_step(group, t)
-                if t == 0 and n == 1:
-                    interleave(before)
-                apply_sign(group, t)
-                if t == 0 and before and before not in interleaved:
-                    interleave(before)
-            if before:
+                if t < LAST_SLOT:
+                    apply_sign(group, t)
+            if before is None:
+                nc.vector.tensor_tensor(
+                    out=sign_ratio[:],
+                    in0=gain_sign[:],
+                    in1=gain_sign[:, :, LAST_SLOT:].to_broadcast([P, PASSES, PACK]),
+                    op=ALU.mult,
+                )
+            else:
                 quantize(before)
             if n in MIX_GROUPS:
                 for e in range(MIX_RUN):
                     i, c = units.pop(0)
-                    finish(i, c, first_mix_pass(i, c), e == MIX_RUN - 1)
-                interleave(group)
+                    z = first_mix_pass(i, c)
+                    mix_pass(i, c, 1, z)
+                    if e == MIX_RUN - 1:
+                        for_vector.append((i, c, z))
+                    else:
+                        empty(i, c, z, False)
         interleave(groups[-1], parts=2)
         quantize(groups[-1], parts=2)
         for i, c in units:

@@ -29,6 +29,7 @@ GROUPS = CHUNKS * PASSES
 BANKS = 8
 SPAN = 256
 PLANE_AT = 128
+ROW_APART = 16
 WARM_UPS = 6
 MIX_GROUPS = (4, 5, 6)
 MIX_RUN = 2
@@ -74,13 +75,13 @@ def tile_filter_bank_channel_mixer_s4_kernel(
         x_plane_first = placed(keep, [P, PASSES, CHUNK], PLANE_AT, "x_plane_first")
         x_plane_rest = placed(keep, [P, PASSES, FRAMES - CHUNK], PLANE_AT, "x_plane_rest")
         mix_plane = placed(keep, [P, PASSES, CHANNELS], PLANE_AT, "mix_plane")
-        gain_bf = keep.tile([P, PASSES, PACK], BF16, name="gain_bf")
+        gain_bf = keep.tile([P, PASSES, ROW_APART], BF16, name="gain_bf")[:, :, 0:PACK]
         gain_f32 = keep.tile([P, PASSES, PACK], F32, name="gain_f32")
         below_zero = keep.tile([P, PASSES, PACK], BF16, name="below_zero")
         gain_sign = keep.tile([P, PASSES, PACK], BF16, name="gain_sign")
         sign_ratio = keep.tile([P, PASSES, PACK], BF16, name="sign_ratio")
         first_abs = once.tile([P, LAST_SLOT, CHUNK], F32, name="first_abs", align_bytes=SPAN)
-        bias_bf = keep.tile([P, C_TILES, 2], BF16, name="bias_bf")
+        bias_bf = keep.tile([P, C_TILES, ROW_APART], BF16, name="bias_bf")
         x_rows_early = keep.tile([P, PASSES, CHUNK], U8, name="x_rows_early", align_bytes=SPAN)
 
         def clear(plane):
@@ -119,7 +120,7 @@ def tile_filter_bank_channel_mixer_s4_kernel(
         for r in range(4):
             load_scale_rows(nc.sync, bank_planes[1], bank_scales, K_PASS, K_PASS, r)
         load_codes(bank_codes[1], bank_words, 2 * K_PASS, 2 * K_PASS)
-        nc.sync.dma_start(out=gain_bf[:], in_=gain.rearrange("(h p t) -> p h t", p=P, t=PACK))
+        nc.sync.dma_start(out=gain_bf, in_=gain.rearrange("(h p t) -> p h t", p=P, t=PACK))
 
         unread = psum.tile([P, CHUNK], F32, name="bank", tag="bank", bufs=BANKS)
         zeros = mix_plane[:].rearrange("p g n -> p (g n)")
@@ -263,9 +264,10 @@ def tile_filter_bank_channel_mixer_s4_kernel(
         for t in range(2):
             deal_codes(nc.vector.tensor_copy, 1, t, t + 1)
         deal_scales(1, 2, PACK)
-        nc.vector.tensor_scalar(out=below_zero[:], in0=gain_bf[:], scalar1=0.0, scalar2=-2.0, op0=ALU.is_lt, op1=ALU.mult)
-        nc.vector.tensor_copy(out=gain_f32[:], in_=gain_bf[:])
-        deal_codes(nc.vector.tensor_copy, 1, 2, PACK)
+        deal_codes(nc.vector.tensor_copy, 1, 2, LAST_SLOT)
+        nc.vector.tensor_copy(out=gain_f32[:], in_=gain_bf)
+        nc.vector.tensor_scalar(out=below_zero[:], in0=gain_bf, scalar1=0.0, scalar2=-2.0, op0=ALU.is_lt, op1=ALU.mult)
+        deal_codes(nc.vector.tensor_copy, 1, LAST_SLOT, PACK)
         nc.vector.tensor_scalar(out=gain_sign[:], in0=below_zero[:], scalar1=1.0, scalar2=None, op0=ALU.add)
 
         last = CHUNKS - 1

@@ -31,7 +31,7 @@ SPAN = 256
 PLANE_AT = 128
 ROW_APART = 16
 WARM_UPS = 6
-MIX_GROUPS = (4, 5, 6)
+MIX_GROUPS = (4, 5)
 MIX_RUN = 2
 AHEAD = 2
 
@@ -77,9 +77,9 @@ def tile_filter_bank_channel_mixer_s4_kernel(
         mix_plane = placed(keep, [P, PASSES, CHANNELS], PLANE_AT, "mix_plane")
         gain_bf = keep.tile([P, PASSES, ROW_APART], BF16, name="gain_bf")[:, :, 0:PACK]
         gain_f32 = keep.tile([P, PASSES, PACK], F32, name="gain_f32")
-        below_zero = keep.tile([P, PASSES, PACK], BF16, name="below_zero")
-        gain_sign = keep.tile([P, PASSES, PACK], BF16, name="gain_sign")
-        sign_ratio = keep.tile([P, PASSES, PACK], BF16, name="sign_ratio")
+        below_zero = keep.tile([P, PASSES, PACK], F32, name="below_zero")
+        gain_sign = keep.tile([P, PASSES, PACK], F32, name="gain_sign")
+        sign_ratio = keep.tile([P, PASSES, PACK], F32, name="sign_ratio")
         first_abs = once.tile([P, LAST_SLOT, CHUNK], F32, name="first_abs", align_bytes=SPAN)
         bias_bf = keep.tile([P, C_TILES, ROW_APART], BF16, name="bias_bf")
         x_rows_early = keep.tile([P, PASSES, CHUNK], U8, name="x_rows_early", align_bytes=SPAN)
@@ -192,7 +192,7 @@ def tile_filter_bank_channel_mixer_s4_kernel(
                 nc.vector.tensor_scalar(
                     out=rows,
                     in0=first_abs[:, t, :],
-                    scalar1=gain_bf[:, h, t : t + 1],
+                    scalar1=gain_f32[:, h, t : t + 1],
                     scalar2=gain_sign[:, h, LAST_SLOT:],
                     op0=ALU.mult,
                     op1=ALU.mult,
@@ -264,10 +264,9 @@ def tile_filter_bank_channel_mixer_s4_kernel(
         for t in range(2):
             deal_codes(nc.vector.tensor_copy, 1, t, t + 1)
         deal_scales(1, 2, PACK)
-        deal_codes(nc.vector.tensor_copy, 1, 2, LAST_SLOT)
-        nc.vector.tensor_copy(out=gain_f32[:], in_=gain_bf)
         nc.vector.tensor_scalar(out=below_zero[:], in0=gain_bf, scalar1=0.0, scalar2=-2.0, op0=ALU.is_lt, op1=ALU.mult)
-        deal_codes(nc.vector.tensor_copy, 1, LAST_SLOT, PACK)
+        nc.vector.tensor_copy(out=gain_f32[:], in_=gain_bf)
+        deal_codes(nc.vector.tensor_copy, 1, 2, PACK)
         nc.vector.tensor_scalar(out=gain_sign[:], in0=below_zero[:], scalar1=1.0, scalar2=None, op0=ALU.add)
 
         last = CHUNKS - 1
@@ -276,7 +275,7 @@ def tile_filter_bank_channel_mixer_s4_kernel(
         for_vector = []
         for n, group in enumerate(groups):
             before = groups[n - 1] if n else None
-            if before:
+            if n == 1:
                 interleave(before)
             if for_vector:
                 empty(*for_vector.pop(), True)
@@ -284,6 +283,8 @@ def tile_filter_bank_channel_mixer_s4_kernel(
                 filter_step(group, t)
                 if t < LAST_SLOT:
                     apply_sign(group, t)
+                if t == 0 and n > 1:
+                    interleave(before)
             if before is None:
                 nc.vector.tensor_tensor(
                     out=sign_ratio[:],

@@ -33,7 +33,7 @@ ROW_APART = 16
 WARM_UPS = 6
 MIX_GROUPS = (4, 5)
 MIX_RUN = 2
-AHEAD = 2
+AHEAD = 1
 
 
 def tile_filter_bank_channel_mixer_s4_kernel(
@@ -147,7 +147,9 @@ def tile_filter_bank_channel_mixer_s4_kernel(
         nc.sync.dma_start(out=mix_codes[:], in_=mix_words.rearrange("g p n t -> p g (n t)"))
         nc.sync.dma_start(out=bias_bf[:, :, 0:1], in_=bias.rearrange("(c p o) -> p c o", p=P, o=1))
         for i in range(2, CHUNKS):
-            load_frames(i)
+            for g in range(PASSES):
+                words = x_words[g, :, 2 * CHUNK * i : 2 * CHUNK * (i + 1)]
+                nc.sync.dma_start(out=x_codes[i][:, g, :].bitcast(I32), in_=words.bitcast(I32))
 
         def deal_codes(move, h, t0, t1):
             move(

from contextlib import ExitStack

import concourse.mybir as mybir

SAMPLES, FRAMES, FILTERS, CHANNELS = 1024, 2048, 1024, 512
FLOPS = 2 * SAMPLES * FRAMES * FILTERS + 2 * FILTERS * FRAMES * CHANNELS

F32 = mybir.dt.float32
BF16 = mybir.dt.bfloat16
I32 = mybir.dt.int32
U32 = mybir.dt.uint32
U16 = mybir.dt.uint16
U8 = mybir.dt.uint8
FP8X4 = mybir.dt.float8_e4m3fn_x4
FP4X4 = mybir.dt.float4_e2m1fn_x4
ALU = mybir.AluOpType
ACT = mybir.ActivationFunctionType

P = 128
PACK = 4
LAST_SLOT = PACK - 1
K_PASS = P * PACK
PASSES = 2
QUADRANT = 32
CHUNK = 512
CHUNKS = FRAMES // CHUNK
C_TILES = CHANNELS // P
GROUPS = CHUNKS * PASSES
BANKS = 8
SPAN = 256
PLANE_AT = 128
ROW_APART = 16
WARM_UPS = 6
MIX_GROUPS = (4, 5)
MIX_RUN = 2
AHEAD = 1


def tile_filter_bank_channel_mixer_s4_kernel(
    tc, x_words, x_scales, bank_words, bank_scales, gain, mix_words, mix_scales, bias, out
):
    nc = tc.nc
    with ExitStack() as ctx:
        keep = ctx.enter_context(tc.tile_pool(name="keep", bufs=1))
        work = ctx.enter_context(tc.tile_pool(name="work", bufs=3))
        once = ctx.enter_context(tc.tile_pool(name="once", bufs=1))
        psum = ctx.enter_context(tc.psum_pool(name="psum", bufs=4))
        ctx.enter_context(nc.allow_non_contiguous_dma(reason="small gain and bias columns"))
        ctx.enter_context(tc.manual_schedule())

        def placed(pool, shape, shift, name, bufs=1):
            size = 1
            for extent in shape[1:]:
                size = size * extent
            room = pool.tile([P, shift + size], U8, name=name, tag=name, bufs=bufs, align_bytes=SPAN)
            names = " ".join("d%d" % e for e in range(len(shape) - 1))
            sizes = {"d%d" % e: extent for e, extent in enumerate(shape[1:])}
            return room[:, shift:].rearrange("p (%s) -> p %s" % (names, names), **sizes)

        x_codes = []
        for i in range(CHUNKS):
            chunk_codes = placed(keep, [P, PASSES, 2 * CHUNK], 0, "x%d" % i)
            x_codes.append(chunk_codes)
        both_planes = keep.tile([P, PASSES, PASSES, K_PASS], U8, name="bank_plane", align_bytes=SPAN)
        bank_planes = [both_planes[:, h] for h in range(PASSES)]
        bank_codes, slot_codes, slot_planes = [], [], []
        for h in range(PASSES):
            as_loaded = keep.tile([P, PASSES, 2 * K_PASS], U8, name="bank_codes%d" % h, align_bytes=SPAN)
            bank_codes.append(as_loaded)
            dealt_codes = placed(keep, [P, PACK, PASSES, 2 * P], 0, "slot_codes%d" % h)
            slot_codes.append(dealt_codes)
            dealt_plane = placed(keep, [P, PACK, PASSES, 2 * P], PLANE_AT, "slot_planes%d" % h)[:, :, :, 0:P]
            slot_planes.append(dealt_plane)
        mix_codes = placed(keep, [P, PASSES, 4 * CHANNELS], 0, "mix_codes")
        x_plane_first = placed(keep, [P, PASSES, CHUNK], PLANE_AT, "x_plane_first")
        x_plane_rest = placed(keep, [P, PASSES, FRAMES - CHUNK], PLANE_AT, "x_plane_rest")
        mix_plane = placed(keep, [P, PASSES, CHANNELS], PLANE_AT, "mix_plane")
        gain_bf = keep.tile([P, PASSES, ROW_APART], BF16, name="gain_bf")[:, :, 0:PACK]
        gain_f32 = keep.tile([P, PASSES, PACK], F32, name="gain_f32")
        below_zero = keep.tile([P, PASSES, PACK], F32, name="below_zero")
        gain_sign = keep.tile([P, PASSES, PACK], F32, name="gain_sign")
        sign_ratio = keep.tile([P, PASSES, PACK], F32, name="sign_ratio")
        first_abs = once.tile([P, LAST_SLOT, CHUNK], F32, name="first_abs", align_bytes=SPAN)
        bias_bf = keep.tile([P, C_TILES, ROW_APART], BF16, name="bias_bf")
        x_rows_early = keep.tile([P, PASSES, CHUNK], U8, name="x_rows_early", align_bytes=SPAN)

        def clear(plane):
            nc.vector.memset(plane[:].rearrange("p g n -> p (g n)").bitcast(I32), 0)

        def load_codes(tile, src, first, count):
            nc.sync.dma_start(
                out=tile[:].bitcast(I32), in_=src[:, :, first : first + count].rearrange("g p b -> p g b").bitcast(I32)
            )

        def load_scale_rows(eng, plane, src, first, count, r):
            eng.dma_start(
                out=plane[r:P:QUADRANT].bitcast(I32),
                in_=src[:, :, first : first + count].rearrange("g (q r) n -> r q g n", r=4)[r].bitcast(I32),
            )

        def load_scale_quadrant(eng, plane, src, count, q):
            eng.dma_start(
                out=plane[QUADRANT * q : QUADRANT * q + 4].bitcast(I32),
                in_=src[:, 4 * q : 4 * q + 4, 0:count].rearrange("g r n -> r g n").bitcast(I32),
            )

        def load_frames(i):
            load_codes(x_codes[i], x_words, 2 * CHUNK * i, 2 * CHUNK)

        load_scale_quadrant(nc.sync, x_rows_early, x_scales, CHUNK, 0)
        load_scale_quadrant(nc.scalar, x_rows_early, x_scales, CHUNK, 2)
        load_codes(bank_codes[0], bank_words, 0, 2 * K_PASS)
        for plane in (bank_planes[0], mix_plane, x_plane_first, bank_planes[1], x_plane_rest):
            clear(plane)
        for r in range(4):
            load_scale_rows(nc.scalar if r % 2 else nc.sync, bank_planes[0], bank_scales, 0, K_PASS, r)
        load_frames(0)
        for q in (1, 3):
            load_scale_quadrant(nc.sync, x_plane_first, x_scales, CHUNK, q)
        for r in range(4):
            load_scale_rows(nc.sync, bank_planes[1], bank_scales, K_PASS, K_PASS, r)
        load_codes(bank_codes[1], bank_words, 2 * K_PASS, 2 * K_PASS)
        nc.sync.dma_start(out=gain_bf, in_=gain.rearrange("(h p t) -> p h t", p=P, t=PACK))

        unread = psum.tile([P, CHUNK], F32, name="bank", tag="bank", bufs=BANKS)
        zeros = mix_plane[:].rearrange("p g n -> p (g n)")
        for e in range(WARM_UPS):
            nc.tensor.matmul_mx(
                out=unread[:],
                lhsT=zeros[:, 0 : 2 * P].bitcast(FP4X4),
                lhsT_scale=zeros[:, 0:P],
                rhs=zeros.bitcast(FP4X4),
                rhs_scale=zeros[:, 0:CHUNK],
                start=True,
                stop=True,
            )

        for q in (0, 2):
            rows = slice(QUADRANT * q, QUADRANT * q + 4)
            nc.vector.tensor_copy(out=x_plane_first[rows].bitcast(I32), in_=x_rows_early[rows].bitcast(I32))

        for r in range(4):
            load_scale_rows(nc.sync, x_plane_rest, x_scales, CHUNK, FRAMES - CHUNK, r)
        load_frames(1)
        for r in range(4):
            load_scale_rows(nc.sync, mix_plane, mix_scales, 0, CHANNELS, r)
        nc.sync.dma_start(out=mix_codes[:], in_=mix_words.rearrange("g p n t -> p g (n t)"))
        nc.sync.dma_start(out=bias_bf[:, :, 0:1], in_=bias.rearrange("(c p o) -> p c o", p=P, o=1))
        for i in range(2, CHUNKS):
            for g in range(PASSES):
                words = x_words[g, :, 2 * CHUNK * i : 2 * CHUNK * (i + 1)]
                nc.sync.dma_start(out=x_codes[i][:, g, :].bitcast(I32), in_=words.bitcast(I32))

        def deal_codes(move, h, t0, t1):
            move(
                out=slot_codes[h][:, t0:t1].bitcast(U16),
                in_=bank_codes[h][:].bitcast(U16).rearrange("p g (m t) -> p t g m", t=PACK)[:, t0:t1],
            )

        def deal_scales(h, t0, t1):
            nc.vector.tensor_copy(
                out=slot_planes[h][:, t0:t1],
                in_=bank_planes[h][:].rearrange("p g (m t) -> p t g m", t=PACK)[:, t0:t1],
            )

        by_slot, interleaved, h_planes = {}, {}, {}

        def filter_step(group, t):
            i, h = group
            y = psum.tile([P, CHUNK], F32, name="bank", tag="bank", bufs=BANKS)
            plane, n0 = (x_plane_first, 0) if i == 0 else (x_plane_rest, CHUNK * (i - 1))
            for g in range(PASSES):
                nc.tensor.matmul_mx(
                    out=y[:],
                    lhsT=slot_codes[h][:, t, g, :].bitcast(FP4X4),
                    lhsT_scale=slot_planes[h][:, t, g, :],
                    rhs=x_codes[i][:, g, :].bitcast(FP4X4),
                    rhs_scale=plane[:, g, n0 : n0 + CHUNK],
                    start=(g == 0),
                    stop=(g == PASSES - 1),
                )
            if t == 0:
                rectified = work.tile([P, PACK, CHUNK], BF16, name="s", tag="s", bufs=GROUPS, align_bytes=SPAN)
                by_slot[group] = rectified
            if group == (0, 0) and t < LAST_SLOT:
                nc.scalar.activation(out=first_abs[:, t, :], in_=y[:], func=ACT.Abs)
            else:
                nc.scalar.activation(out=by_slot[group][:, t, :], in_=y[:], func=ACT.Abs, scale=gain_f32[:, h, t : t + 1])

        def apply_sign(group, t):
            h = group[1]
            rows = by_slot[group][:, t, :]
            if group == (0, 0):
                nc.vector.tensor_scalar(
                    out=rows,
                    in0=first_abs[:, t, :],
                    scalar1=gain_f32[:, h, t : t + 1],
                    scalar2=gain_sign[:, h, LAST_SLOT:],
                    op0=ALU.mult,
                    op1=ALU.mult,
                )
            else:
                nc.vector.tensor_scalar(
                    out=rows, in0=rows, scalar1=sign_ratio[:, h, t : t + 1], scalar2=None, op0=ALU.mult
                )

        def interleave(group, parts=1):
            words = work.tile([P, CHUNK, PACK], BF16, name="gr", tag="gr", bufs=GROUPS, align_bytes=SPAN)
            for e in range(parts):
                cols = slice(e * CHUNK // parts, (e + 1) * CHUNK // parts)
                nc.vector.tensor_scalar(
                    out=words[:, cols, :].rearrange("p (c i) t -> p c t i", i=4),
                    in0=by_slot[group][:, :, cols].rearrange("p t (c i) -> p c t i", i=4),
                    scalar1=gain_sign[:, group[1], LAST_SLOT:],
                    scalar2=None,
                    op0=ALU.mult,
                )
            interleaved[group] = words

        def quantize(group, parts=1):
            codes = placed(work, [P, 4 * CHUNK], 0, "hc", GROUPS).bitcast(U32)
            plane = placed(work, [P, CHUNK], PLANE_AT, "hs", GROUPS)
            h_planes[group] = (codes, plane)
            for e in range(parts):
                cols = slice(e * CHUNK // parts, (e + 1) * CHUNK // parts)
                nc.vector.quantize_mx(
                    out=codes[:, cols].bitcast(FP8X4),
                    scales=plane[:, cols],
                    in_=interleaved[group][:, cols, :].rearrange("p n t -> p (n t)"),
                )

        def mix_pass(i, c, h, z):
            codes, plane = h_planes[(i, h)]
            nc.tensor.matmul_mx(
                out=z[:],
                lhsT=mix_codes[:, h, 4 * P * c : 4 * P * (c + 1)].bitcast(FP8X4),
                lhsT_scale=mix_plane[:, h, P * c : P * (c + 1)],
                rhs=codes.bitcast(FP8X4),
                rhs_scale=plane,
                start=(h == 0),
                stop=(h == PASSES - 1),
            )

        def first_mix_pass(i, c):
            z = psum.tile([P, CHUNK], F32, name="bank", tag="bank", bufs=BANKS)
            mix_pass(i, c, 0, z)
            return z

        def empty(i, c, z, on_vector):
            result = work.tile([P, CHUNK], F32, name="o", tag="o", bufs=CHUNKS * C_TILES, align_bytes=SPAN)
            if on_vector:
                nc.vector.tensor_scalar(out=result[:], in0=z[:], scalar1=bias_bf[:, c, 0:1], scalar2=None, op0=ALU.add)
            else:
                nc.scalar.activation(out=result[:], in_=z[:], func=ACT.Identity, bias=bias_bf[:, c, 0:1])
            nc.sync.dma_start(out=out[P * c : P * (c + 1), CHUNK * i : CHUNK * (i + 1)], in_=result[:])

        def finish(i, c, z, on_vector):
            mix_pass(i, c, 1, z)
            empty(i, c, z, on_vector)

        for t in range(PACK):
            deal_codes(nc.scalar.copy, 0, t, t + 1)
        for t0, t1 in ((0, 1), (1, 2), (2, PACK)):
            deal_scales(0, t0, t1)
        deal_scales(1, 0, 2)
        for t in range(2):
            deal_codes(nc.vector.tensor_copy, 1, t, t + 1)
        deal_scales(1, 2, PACK)
        nc.vector.tensor_scalar(out=below_zero[:], in0=gain_bf, scalar1=0.0, scalar2=-2.0, op0=ALU.is_lt, op1=ALU.mult)
        nc.vector.tensor_copy(out=gain_f32[:], in_=gain_bf)
        deal_codes(nc.vector.tensor_copy, 1, 2, PACK)
        nc.vector.tensor_scalar(out=gain_sign[:], in0=below_zero[:], scalar1=1.0, scalar2=None, op0=ALU.add)

        last = CHUNKS - 1
        groups = [(i, h) for i in range(CHUNKS) for h in range(PASSES)]
        units = [(i, c) for i in range(last) for c in range(C_TILES)]
        for_vector = []
        for n, group in enumerate(groups):
            before = groups[n - 1] if n else None
            if n == 1:
                interleave(before)
            if for_vector:
                empty(*for_vector.pop(), True)
            for t in range(PACK):
                filter_step(group, t)
                if t < LAST_SLOT:
                    apply_sign(group, t)
                if t == 0 and n > 1:
                    interleave(before)
            if before is None:
                nc.vector.tensor_tensor(
                    out=sign_ratio[:],
                    in0=gain_sign[:],
                    in1=gain_sign[:, :, LAST_SLOT:].to_broadcast([P, PASSES, PACK]),
                    op=ALU.mult,
                )
            else:
                quantize(before)
            if n in MIX_GROUPS:
                for e in range(MIX_RUN):
                    i, c = units.pop(0)
                    z = first_mix_pass(i, c)
                    mix_pass(i, c, 1, z)
                    if e == MIX_RUN - 1:
                        for_vector.append((i, c, z))
                    else:
                        empty(i, c, z, False)
        interleave(groups[-1], parts=2)
        quantize(groups[-1], parts=2)
        for i, c in units:
            finish(i, c, first_mix_pass(i, c), False)

        ahead = [first_mix_pass(last, c) for c in range(AHEAD)]
        for c in range(C_TILES):
            finish(last, c, ahead[c] if c < AHEAD else first_mix_pass(last, c), c % 2 == 0)
